import numpy as np
import ml_dtypes


def mxq(x, axis, fmt="e4m3"):
    dtype, down = {"e4m3": (ml_dtypes.float8_e4m3fn, 7), "e5m2": (ml_dtypes.float8_e5m2, 14)}[fmt]
    v = np.moveaxis(np.asarray(x, np.float32).astype(ml_dtypes.bfloat16).astype(np.float64), axis, -1)
    blocks = v.reshape(v.shape[:-1] + (-1, 32))
    amax = np.abs(blocks).max(-1, keepdims=True)
    byte = np.maximum(np.where(amax > 0, np.frexp(amax)[1] - 1 + 127, 0) - down, 1)
    scale = np.exp2(byte - 127.0)
    codes = (blocks / scale).astype(np.float32).astype(dtype).astype(np.float64)
    return np.moveaxis((codes * scale).reshape(v.shape), -1, axis)


WIDE = False


def mx_kscale(k):
    if not WIDE:
        return np.ones(k)
    levels = np.array([10, -10, 5, -5, 0])
    if k % 512:
        return np.exp2(np.random.permutation(np.resize(levels, k // 32))).repeat(32)
    a = np.empty((k // 512, 16))
    for p in range(k // 512):
        a[p, :8] = np.random.permutation(np.resize(levels, 8))
        for g in range(8):
            far = levels[np.abs(levels - a[p, g]) >= 10]
            a[p, g + 8] = far[np.random.randint(len(far))]
    return np.exp2(a.ravel()).repeat(32)


BF16 = ml_dtypes.bfloat16


def bf(x):
    return np.asarray(x, np.float32).astype(BF16)


def f64(x):
    return np.asarray(x).astype(np.float64)

E4M3FN = np.array([(-1.0 if i & 128 else 1.0) * ((1.0 + (i & 7) / 8.0) * 2.0 ** (((i >> 3) & 15) - 7) if i & 120 else (i & 7) * 2.0 ** -9) for i in range(256)])


def e4m3fn_bytes(y):
    return np.clip(np.asarray(y, np.float64), -448.0, 448.0).astype(np.float32).astype(ml_dtypes.float8_e4m3fn).view(np.uint8)


def e4m3fn_values(b):
    return E4M3FN[b]


T, K, N, B = 2048, 1536, 1024, 128


def setup_inputs():
    f = mx_kscale(K)
    ret = np.random.standard_normal((T, K)) * f
    ret_scale = (np.abs(ret.reshape(T, K // B, B)).max(axis=2) / 448.0).astype(np.float32)
    ret_bytes = e4m3fn_bytes(ret / np.repeat(f64(ret_scale), B, axis=1))
    size = np.random.uniform(0.5, 1.5, (N, 1))
    pos = size * np.random.standard_normal((N, K)) / np.sqrt(K) / f
    rate = np.random.uniform(0.2, 1.0, K) / np.sqrt(K) * f
    return {"ret_bytes": ret_bytes,
            "ret_scale": ret_scale,
            "pos": bf(pos),
            "rate": bf(rate)}


def reference(ret_bytes, ret_scale, pos, rate):
    ret = e4m3fn_values(ret_bytes) * np.repeat(f64(ret_scale), B, axis=1)
    p = f64(pos)
    gross = mxq(ret, 1, "e4m3") @ mxq(p, 1, "e4m3").T
    cost = (np.abs(p) * f64(rate)).sum(axis=1)
    return gross - cost

@@ -1,0 +1,409 @@
+from contextlib import ExitStack
+
+import concourse.mybir as mybir
+from concourse.masks import make_identity
+
+T, K, N = 2048, 1536, 1024
+FLOPS = 2 * T * K * N + 3 * N * K
+
+F32 = mybir.dt.float32
+BF16 = mybir.dt.bfloat16
+U32 = mybir.dt.uint32
+I32 = mybir.dt.int32
+U8 = mybir.dt.uint8
+FP8 = mybir.dt.float8_e4m3fn
+FP8X4 = mybir.dt.float8_e4m3fn_x4
+ALU = mybir.AluOpType
+COPY = mybir.ActivationFunctionType.Copy
+
+P = 128
+G = K // 512
+BLOCKS = K // 128
+TILES = T // P
+PAIRS = TILES // 2
+POS_PAIRS = N // 256
+MANUAL = True
+PERM_FROM = 4
+GA = [3, 3, 3, 3, 3, 3, 3, 3]
+
+
+def tile_scenario_profit_after_cost_d1_kernel(tc, ret_bytes, ret_scale, pos, rate, out):
+    nc = tc.nc
+    with ExitStack() as ctx:
+        const = ctx.enter_context(tc.tile_pool(name="const", bufs=1))
+        work = ctx.enter_context(tc.tile_pool(name="work", bufs=3))
+        psum = ctx.enter_context(tc.psum_pool(name="psum", bufs=4))
+        if MANUAL:
+            ctx.enter_context(tc.manual_schedule())
+
+        ident = const.tile([P, P], F32, name="ident")
+        make_identity(nc, ident[:])
+
+        bytes_v = ret_bytes.rearrange("(p i) k -> p i k", i=TILES)
+        out_v = out.rearrange("(p i) n -> p i n", i=TILES)
+
+        rate_sb = const.tile([P, G, 4], BF16, name="rate_sb")
+        scale_sb = const.tile([P, TILES, BLOCKS], F32, name="scale_sb")
+        pos_sb = [const.tile([P, 2, K], BF16, name=f"pos_sb{c}", align_bytes=64) for c in range(POS_PAIRS)]
+        ret_u8 = [const.tile([P, 2, K], U8, name=f"ret_u8_{i}", align_bytes=64) for i in range(PAIRS)]
+
+        nc.scalar.dma_start(out=scale_sb[:], in_=ret_scale.rearrange("(p i) b -> p i b", i=TILES))
+        nc.scalar.dma_start(out=rate_sb[:], in_=rate.rearrange("(g p t) -> p g t", p=P, t=4))
+        pos_tile_v = pos.rearrange("(c s r) k -> c s r k", s=2, r=P)
+
+        def load_pos(c, s):
+            if c == 0 and s == 0:
+                for g in range(G):
+                    cols = slice(512 * g, 512 * g + 512)
+                    nc.sync.dma_start(out=pos_sb[c][:, s, cols], in_=pos_tile_v[c, s][:, cols])
+            else:
+                nc.sync.dma_start(out=pos_sb[c][:, s], in_=pos_tile_v[c, s])
+
+        def load_ret(i):
+            nc.sync.dma_start(out=ret_u8[i][:], in_=bytes_v[:, 2 * i : 2 * i + 2, :])
+
+
+        pos_q = const.tile([P, G, N], U32, name="pos_q", align_bytes=64)
+        pos_s = const.tile([P, G, N], U8, name="pos_s", align_bytes=64)
+        pos_abs = const.tile([P, POS_PAIRS, G, 2, 256], I32, name="pos_abs", align_bytes=64)
+        cost_col = const.tile([P, N // P], F32, name="cost_col")
+        cost_bc = const.tile([P, N], F32, name="cost_bc", align_bytes=64)
+
+        grouped = {}
+        banks = {}
+
+        def pos_transpose(c, s, tag):
+            words = pos_sb[c][:].bitcast(F32)
+            if s == 0:
+                for g in range(G):
+                    banks["pos", c, g] = psum.tile([P, 2, 256], F32, name=tag, tag=tag, bufs=4)
+            for g in range(G):
+                for u in range(2):
+                    nc.tensor.transpose(
+                        banks["pos", c, g][:, u, P * s : P * s + P], words[:, s, 256 * g + u : 256 * g + 256 : 2], ident[:]
+                    )
+
+        def copy_out(key, tag, bufs, copy=None):
+            tile = work.tile([P, 256, 4], BF16, name=tag, tag=tag, bufs=bufs, align_bytes=64)
+            (copy or nc.scalar.copy)(
+                out=tile[:].rearrange("p r t -> p (r t)").bitcast(F32).rearrange("p (r u) -> p r u", u=2),
+                in_=banks[key][:].rearrange("p u r -> p r u"),
+            )
+            grouped[key] = tile
+
+        def pos_copy(c, g):
+            copy_out(("pos", c, g), "pos_grp", 6)
+
+        def pos_copy_v(c, g):
+            copy_out(("pos", c, g), "pos_grp", 6, nc.vector.tensor_copy)
+
+        def pos_quantize(c, g):
+            cols = slice(256 * c, 256 * c + 256)
+            nc.vector.quantize_mx(
+                out=pos_q[:, g, cols].bitcast(FP8X4),
+                scales=pos_s[:, g, cols],
+                in_=grouped["pos", c, g][:].rearrange("p r t -> p (r t)"),
+            )
+
+        def pos_absolute(c, g):
+            nc.vector.tensor_scalar(
+                out=pos_abs[:, c, g],
+                in0=grouped["pos", c, g][:].rearrange("p r t -> p (r t)").bitcast(I32).rearrange("p (r u) -> p u r", u=2),
+                scalar1=0x7FFF7FFF,
+                scalar2=None,
+                op0=ALU.bitwise_and,
+            )
+
+        cost_ps = {}
+
+        def cost_sum(c, tag):
+            cost_ps[c] = psum.tile([P, 2], F32, name=tag, tag=tag, bufs=4)
+            for s in range(2):
+                for k in range(4 * G):
+                    g, t = k // 4, k % 4
+                    u, e = t // 2, t % 2
+                    mags = pos_abs[:, c, g, u].bitcast(BF16)
+                    nc.tensor.matmul(
+                        out=cost_ps[c][:, s : s + 1],
+                        lhsT=mags[:, 256 * s + e : 256 * s + 256 : 2],
+                        rhs=rate_sb[:, g, t : t + 1],
+                        start=(k == 0),
+                        stop=(k == 4 * G - 1),
+                    )
+
+        def cost_spread_tensor(h, tag):
+            bank = psum.tile([P, 512], F32, name=tag, tag=tag, bufs=4)
+            for m in range(4):
+                col = 4 * h + m
+                nc.tensor.transpose(bank[:, P * m : P * m + P], cost_col[:, col : col + 1].to_broadcast([P, P]), ident[:])
+            banks["cost", h] = bank
+
+        def cost_spread_copy(h):
+            nc.scalar.copy(out=cost_bc[:, 512 * h : 512 * h + 512], in_=banks["cost", h][:])
+
+        wide = {}
+
+        def new_wide(i):
+            if (i, 0) in wide:
+                return
+            wide[i, 0] = work.tile([P, K], BF16, name="wide_a", tag="wide_a", bufs=4, align_bytes=64)
+            wide[i, 1] = work.tile([P, K], BF16, name="wide_b", tag="wide_b", bufs=4, align_bytes=64)
+
+        def widen_a(i, first, last):
+            dst = wide[i, 0][:].rearrange("r (g u p e) -> r g p u e", g=G, u=2, e=2)
+            for b in range(first, last):
+                q = b % 4
+                if b // 4 >= GA[i]:
+                    nc.scalar.activation(
+                        out=wide[i, 0][:, P * b : P * b + P],
+                        in_=ret_u8[i][:, 0, P * b : P * b + P].bitcast(FP8),
+                        func=COPY,
+                        scale=scale_sb[:, 2 * i, b : b + 1],
+                    )
+                    continue
+                nc.vector.tensor_scalar(
+                    out=dst[:, b // 4, 32 * q : 32 * q + 32],
+                    in0=ret_u8[i][:, 0, P * b : P * b + P].bitcast(FP8).rearrange("r (p u e) -> r p u e", u=2, e=2),
+                    scalar1=scale_sb[:, 2 * i, b : b + 1],
+                    scalar2=None,
+                    op0=ALU.mult,
+                )
+
+        def widen_b(i, first, last):
+            for b in range(first, last):
+                nc.scalar.activation(
+                    out=wide[i, 1][:, P * b : P * b + P],
+                    in_=ret_u8[i][:, 1, P * b : P * b + P].bitcast(FP8),
+                    func=COPY,
+                    scale=scale_sb[:, 2 * i + 1, b : b + 1],
+                )
+
+        def widen_b_v(i, first, last):
+            for b in range(first, last):
+                nc.vector.tensor_scalar(
+                    out=wide[i, 1][:, P * b : P * b + P],
+                    in0=ret_u8[i][:, 1, P * b : P * b + P].bitcast(FP8),
+                    scalar1=scale_sb[:, 2 * i + 1, b : b + 1],
+                    scalar2=None,
+                    op0=ALU.mult,
+                )
+
+        def permute_b(i):
+            perm[i] = work.tile([P, K], BF16, name="perm_b", tag="perm_b", bufs=3, align_bytes=64)
+            nc.scalar.copy(
+                out=perm[i][:].bitcast(F32).rearrange("r (g u p) -> r g u p", g=G, u=2),
+                in_=wide[i, 1][:].bitcast(F32).rearrange("r (g p u) -> r g u p", g=G, u=2),
+            )
+
+        perm = {}
+
+        def ret_transpose(i, g, tag="tp"):
+            words_a = wide[i, 0][:].bitcast(F32)
+            words_b = (perm[i] if i >= PERM_FROM else wide[i, 1])[:].bitcast(F32)
+            for g in (g,):
+                bank = psum.tile([P, 2, 256], F32, name=tag, tag=tag, bufs=4)
+                for u in range(2):
+                    a_cols = slice(256 * g + P * u, 256 * g + P * u + P) if g < GA[i] else slice(256 * g + u, 256 * g + 256, 2)
+                    nc.tensor.transpose(bank[:, u, 0:P], words_a[:, a_cols], ident[:])
+                for u in range(2):
+                    cols = slice(256 * g + P * u, 256 * g + P * u + P) if i >= PERM_FROM else slice(256 * g + u, 256 * g + 256, 2)
+                    nc.tensor.transpose(bank[:, u, P : 2 * P], words_b[:, cols], ident[:])
+                banks["ret", i, g] = bank
+
+        def ret_copy(i, g):
+            copy_out(("ret", i, g), "ret_grp", 6)
+
+        def ret_copy_v(i, g):
+            copy_out(("ret", i, g), "ret_grp", 6, nc.vector.tensor_copy)
+
+        ret_q = {}
+        ret_s = {}
+
+        def new_ret_q(i):
+            ret_q[i] = work.tile([P, G, 256], U32, name="ret_q", tag="ret_q", bufs=3, align_bytes=64)
+            ret_s[i] = work.tile([P, G, 256], U8, name="ret_s", tag="ret_s", bufs=3, align_bytes=64)
+
+        def ret_quantize(i, g):
+            nc.vector.quantize_mx(
+                out=ret_q[i][:, g].bitcast(FP8X4),
+                scales=ret_s[i][:, g],
+                in_=grouped["ret", i, g][:].rearrange("p r t -> p (r t)"),
+            )
+
+        sums = {}
+
+        def product(i, s, h, n0=0, n=512):
+            acc = psum.tile([P, n], F32, name="mx", tag="mx", bufs=4)
+            for g in range(G):
+                nc.tensor.matmul_mx(
+                    out=acc[:],
+                    lhsT=ret_q[i][:, g, P * s : P * s + P].bitcast(FP8X4),
+                    lhsT_scale=ret_s[i][:, g, P * s : P * s + P],
+                    rhs=pos_q[:, g, 512 * h + n0 : 512 * h + n0 + n].bitcast(FP8X4),
+                    rhs_scale=pos_s[:, g, 512 * h + n0 : 512 * h + n0 + n],
+                    start=(g == 0),
+                    stop=(g == G - 1),
+                )
+            sums[i, s, h, n0] = acc
+
+        result = {}
+
+        def finish(i, s, h, n0=0, n=512):
+            if h == 0:
+                result[i, s] = work.tile([P, N], F32, name="res", tag="res", bufs=6, align_bytes=64)
+            cols = slice(512 * h + n0, 512 * h + n0 + n)
+            nc.vector.tensor_tensor(out=result[i, s][:, cols], in0=sums[i, s, h, n0][:], in1=cost_bc[:, cols], op=ALU.subtract)
+            if i == PAIRS - 1 and s == 1:
+                nc.sync.dma_start(out=out_v[:, 2 * i + s, cols], in_=result[i, s][:, cols])
+            elif h == 1 and n0 + n == 512:
+                nc.sync.dma_start(out=out_v[:, 2 * i + s, :], in_=result[i, s][:])
+
+        def pos_copies(c, nv):
+            for g in range(G):
+                (pos_copy_v if g >= G - nv else pos_copy)(c, g)
+
+        def ret_copies(i, nv):
+            for g in range(G):
+                (ret_copy_v if g >= G - nv else ret_copy)(i, g)
+
+        def pos_codes(c):
+            for g in range(G):
+                pos_quantize(c, g)
+
+        def pos_magnitudes(c):
+            for g in range(G):
+                pos_absolute(c, g)
+
+        def widen_a12(i):
+            new_wide(i)
+            widen_a(i, 0, BLOCKS)
+
+        def widen_b12(i, nv):
+            new_wide(i)
+            widen_b(i, 0, BLOCKS - nv)
+            widen_b_v(i, BLOCKS - nv, BLOCKS)
+            if i >= PERM_FROM:
+                permute_b(i)
+
+        def ret_transposes(i, tag):
+            for g in range(G):
+                ret_transpose(i, g, tag)
+
+        def ret_codes(i):
+            new_ret_q(i)
+            for g in range(G):
+                ret_quantize(i, g)
+
+        def cost_column(c):
+            nc.vector.tensor_copy(out=cost_col[:, 2 * c : 2 * c + 2], in_=cost_ps[c][:])
+
+        load_ret(0)
+        load_pos(0, 0)
+        load_pos(0, 1)
+        load_pos(1, 0)
+        load_ret(1)
+        load_pos(1, 1)
+        load_pos(2, 0)
+        load_pos(2, 1)
+        load_pos(3, 0)
+        load_pos(3, 1)
+        load_ret(2)
+        load_ret(3)
+        load_ret(4)
+        load_ret(5)
+        load_ret(6)
+        load_ret(7)
+        widen_b12(0, 0)
+        pos_transpose(0, 0, "tp")
+        pos_transpose(0, 1, "mx")
+        widen_a12(0)
+        ret_transposes(0, "tp")
+        pos_copies(0, 1)
+        pos_magnitudes(0)
+        pos_transpose(1, 0, "mx")
+        pos_transpose(1, 1, "tp")
+        ret_copies(0, 0)
+        widen_a12(1)
+        ret_codes(0)
+        cost_sum(0, "tp")
+        pos_codes(0)
+        pos_transpose(2, 0, "tp")
+        pos_transpose(3, 0, "mx")
+        pos_transpose(2, 1, "tp")
+        pos_copies(1, 0)
+        pos_magnitudes(1)
+        widen_b12(1, 0)
+        pos_transpose(3, 1, "tp")
+        pos_codes(1)
+        pos_copies(3, 0)
+        cost_sum(1, "mx")
+        pos_copies(2, 1)
+        ret_transposes(1, "mx")
+        cost_column(0)
+        product(0, 0, 0)
+        ret_copies(1, 0)
+        product(0, 1, 0)
+        cost_column(1)
+        cost_spread_tensor(0, "tp")
+        pos_magnitudes(3)
+        cost_spread_copy(0)
+        pos_codes(2)
+        cost_sum(3, "tp")
+        pos_magnitudes(2)
+        ret_codes(1)
+        cost_sum(2, "tp")
+        product(1, 0, 0)
+        pos_codes(3)
+        product(1, 1, 0)
+        finish(0, 0, 0)
+        cost_column(3)
+        product(0, 0, 1)
+        finish(0, 1, 0)
+        widen_b12(2, 0)
+        cost_column(2)
+        product(1, 0, 1)
+        widen_b12(3, 0)
+        cost_spread_tensor(1, "tp")
+        widen_a12(2)
+        ret_transposes(2, "tp")
+        cost_spread_copy(1)
+        finish(1, 0, 0)
+        widen_a12(3)
+        ret_transposes(3, "tp")
+        finish(0, 0, 1)
+        finish(1, 1, 0)
+        ret_copies(2, 0)
+        finish(1, 0, 1)
+        product(1, 1, 1)
+        product(0, 1, 1)
+        ret_codes(2)
+        widen_b12(4, 0)
+        finish(1, 1, 1)
+        finish(0, 1, 1)
+        ret_copies(3, 0)
+        widen_a12(4)
+
+        for i in range(2, PAIRS):
+            far = i + 2
+            if i + 1 < PAIRS:
+                ret_codes(i + 1)
+            for s in range(2):
+                for h in range(2):
+                    if i == PAIRS - 1 and s == 1 and h == 1:
+                        for n0 in (0, 256):
+                            product(i, s, h, n0, 256)
+                            finish(i, s, h, n0, 256)
+                    else:
+                        product(i, s, h)
+                        finish(i, s, h)
+            if far < PAIRS:
+                ret_transposes(far, "tp")
+                if far + 1 < PAIRS:
+                    new_wide(far + 1)
+                    widen_b(far + 1, 0, 8)
+                ret_copies(far, 0)
+                if far + 1 < PAIRS:
+                    widen_b(far + 1, 8, 12)
+                    if far + 1 >= PERM_FROM:
+                        permute_b(far + 1)
+                    widen_a(far + 1, 0, BLOCKS)

@@ -21,10 +21,8 @@ G = K // 512
 BLOCKS = K // 128
 TILES = T // P
 PAIRS = TILES // 2
-POS_PAIRS = N // 256
-MANUAL = True
-PERM_FROM = 4
-GA = [3, 3, 3, 3, 3, 3, 3, 3]
+POS_TILES = N // P
+HALF_WORDS = K // 4
 
 
 def tile_scenario_profit_after_cost_d1_kernel(tc, ret_bytes, ret_scale, pos, rate, out):
@@ -32,378 +30,354 @@ def tile_scenario_profit_after_cost_d1_kernel(tc, ret_bytes, ret_scale, pos, rat
     with ExitStack() as ctx:
         const = ctx.enter_context(tc.tile_pool(name="const", bufs=1))
         work = ctx.enter_context(tc.tile_pool(name="work", bufs=3))
-        psum = ctx.enter_context(tc.psum_pool(name="psum", bufs=4))
-        if MANUAL:
-            ctx.enter_context(tc.manual_schedule())
+        psum = ctx.enter_context(tc.psum_pool(name="psum", bufs=1))
+        ctx.enter_context(tc.manual_schedule())
 
         ident = const.tile([P, P], F32, name="ident")
-        make_identity(nc, ident[:])
-
-        bytes_v = ret_bytes.rearrange("(p i) k -> p i k", i=TILES)
-        out_v = out.rearrange("(p i) n -> p i n", i=TILES)
-
-        rate_sb = const.tile([P, G, 4], BF16, name="rate_sb")
+        rate_rows = const.tile([P, 2 * P], BF16, name="rate_rows")
+        rate_sb = const.tile([P, 2 * G], F32, name="rate_sb")
         scale_sb = const.tile([P, TILES, BLOCKS], F32, name="scale_sb")
-        pos_sb = [const.tile([P, 2, K], BF16, name=f"pos_sb{c}", align_bytes=64) for c in range(POS_PAIRS)]
-        ret_u8 = [const.tile([P, 2, K], U8, name=f"ret_u8_{i}", align_bytes=64) for i in range(PAIRS)]
-
-        nc.scalar.dma_start(out=scale_sb[:], in_=ret_scale.rearrange("(p i) b -> p i b", i=TILES))
-        nc.scalar.dma_start(out=rate_sb[:], in_=rate.rearrange("(g p t) -> p g t", p=P, t=4))
-        pos_tile_v = pos.rearrange("(c s r) k -> c s r k", s=2, r=P)
-
-        def load_pos(c, s):
-            if c == 0 and s == 0:
-                for g in range(G):
-                    cols = slice(512 * g, 512 * g + 512)
-                    nc.sync.dma_start(out=pos_sb[c][:, s, cols], in_=pos_tile_v[c, s][:, cols])
-            else:
-                nc.sync.dma_start(out=pos_sb[c][:, s], in_=pos_tile_v[c, s])
-
-        def load_ret(i):
-            nc.sync.dma_start(out=ret_u8[i][:], in_=bytes_v[:, 2 * i : 2 * i + 2, :])
-
-
+        pos_sb = [const.tile([P, K], BF16, name=f"pos_sb{m}", align_bytes=64) for m in range(POS_TILES)]
+        ret_u8 = [const.tile([P, 2 * K], U8, name=f"ret_u8_{i}", align_bytes=64) for i in range(PAIRS)]
         pos_q = const.tile([P, G, N], U32, name="pos_q", align_bytes=64)
         pos_s = const.tile([P, G, N], U8, name="pos_s", align_bytes=64)
-        pos_abs = const.tile([P, POS_PAIRS, G, 2, 256], I32, name="pos_abs", align_bytes=64)
-        cost_col = const.tile([P, N // P], F32, name="cost_col")
+        pos_abs = const.tile([P, POS_TILES // 2, G, 2, 256], I32, name="pos_abs", align_bytes=64)
+        cost_col = const.tile([P, POS_TILES], F32, name="cost_col")
         cost_bc = const.tile([P, N], F32, name="cost_bc", align_bytes=64)
 
-        grouped = {}
-        banks = {}
+        bytes_v = ret_bytes.rearrange("(p i s) k -> p i (s k)", i=PAIRS, s=2)
+        out_v = out.rearrange("(p i) n -> p i n", i=TILES)
+        pos_v = pos.rearrange("(m r) k -> m r k", r=P)
+        rate_v = rate.rearrange("(g b u w) -> g u b w", g=G, u=2, w=16)
 
-        def pos_transpose(c, s, tag):
-            words = pos_sb[c][:].bitcast(F32)
-            if s == 0:
-                for g in range(G):
-                    banks["pos", c, g] = psum.tile([P, 2, 256], F32, name=tag, tag=tag, bufs=4)
-            for g in range(G):
-                for u in range(2):
-                    nc.tensor.transpose(
-                        banks["pos", c, g][:, u, P * s : P * s + P], words[:, s, 256 * g + u : 256 * g + 256 : 2], ident[:]
-                    )
+        def new_bank(n):
+            return psum.tile([P, 512], F32, name=f"bank{n}", tag=f"bank{n}")
 
-        def copy_out(key, tag, bufs, copy=None):
-            tile = work.tile([P, 256, 4], BF16, name=tag, tag=tag, bufs=bufs, align_bytes=64)
-            (copy or nc.scalar.copy)(
-                out=tile[:].rearrange("p r t -> p (r t)").bitcast(F32).rearrange("p (r u) -> p r u", u=2),
-                in_=banks[key][:].rearrange("p u r -> p r u"),
+        def load_pos(m):
+            nc.sync.dma_start(out=pos_sb[m][:], in_=pos_v[m])
+
+        def load_ret(i):
+            nc.sync.dma_start(out=ret_u8[i][:], in_=bytes_v[:, i])
+
+        def split_halves(engine_copy, dst, src):
+            engine_copy(
+                out=dst.bitcast(F32).rearrange("r (u b w) -> r u b w", u=2, w=8),
+                in_=src.bitcast(F32).rearrange("r (b u w) -> r u b w", u=2, w=8),
             )
-            grouped[key] = tile
 
-        def pos_copy(c, g):
-            copy_out(("pos", c, g), "pos_grp", 6)
+        halved = {}
+        banks = {}
+        bank_of = {}
+        grouped = {}
 
-        def pos_copy_v(c, g):
-            copy_out(("pos", c, g), "pos_grp", 6, nc.vector.tensor_copy)
+        def pos_split(m, engine_copy):
+            halved["pos", m] = work.tile([P, K], BF16, name="pos_halved", tag="pos_halved", bufs=4, align_bytes=64)
+            split_halves(engine_copy, halved["pos", m][:], pos_sb[m][:])
+
+        def claim(kind, pair, numbers):
+            for g in range(G):
+                bank_of[kind, pair, g] = numbers[g]
+
+        def turn(kind, pair, g, s, words, plane):
+            if (kind, pair, g) not in banks:
+                banks[kind, pair, g] = new_bank(bank_of[kind, pair, g])
+            for u in range(2):
+                col = 256 * u + P * s
+                nc.tensor.transpose(banks[kind, pair, g][:, col : col + P], words[:, plane * u : plane * u + P], ident[:])
+
+        def pos_turn(m, passes=range(G)):
+            words = halved["pos", m][:].bitcast(F32)
+            for g in passes:
+                turn("pos", m // 2, g, m % 2, words[:, P * g :], HALF_WORDS)
+
+        def pos_turn_pair(c):
+            for g in range(G):
+                pos_turn(2 * c, (g,))
+                pos_turn(2 * c + 1, (g,))
+
+        def ret_turn(i, passes=range(G)):
+            for g in passes:
+                words = halved["ret", i, g][:].bitcast(F32)
+                for s in range(2):
+                    turn("ret", i, g, s, words[:, 256 * s :], P)
+
+        def copy_out(kind, pair, g, engine_copy):
+            tile = work.tile([P, 1024], BF16, name="grouped", tag="grouped", bufs=8, align_bytes=64)
+            engine_copy(
+                out=tile[:].bitcast(F32).rearrange("p (r u) -> p r u", u=2),
+                in_=banks[kind, pair, g][:].rearrange("p (u r) -> p r u", u=2),
+            )
+            grouped[kind, pair, g] = tile
 
         def pos_quantize(c, g):
             cols = slice(256 * c, 256 * c + 256)
-            nc.vector.quantize_mx(
-                out=pos_q[:, g, cols].bitcast(FP8X4),
-                scales=pos_s[:, g, cols],
-                in_=grouped["pos", c, g][:].rearrange("p r t -> p (r t)"),
-            )
+            nc.vector.quantize_mx(out=pos_q[:, g, cols].bitcast(FP8X4), scales=pos_s[:, g, cols], in_=grouped["pos", c, g][:])
 
         def pos_absolute(c, g):
             nc.vector.tensor_scalar(
                 out=pos_abs[:, c, g],
-                in0=grouped["pos", c, g][:].rearrange("p r t -> p (r t)").bitcast(I32).rearrange("p (r u) -> p u r", u=2),
+                in0=grouped["pos", c, g][:].bitcast(I32).rearrange("p (r u) -> p u r", u=2),
                 scalar1=0x7FFF7FFF,
                 scalar2=None,
                 op0=ALU.bitwise_and,
             )
 
-        cost_ps = {}
+        def rate_turn(n):
+            bank = new_bank(n)
+            nc.tensor.transpose(bank[:, 0:P], rate_rows[:].bitcast(F32), ident[:])
+            banks["rate"] = bank
 
-        def cost_sum(c, tag):
-            cost_ps[c] = psum.tile([P, 2], F32, name=tag, tag=tag, bufs=4)
+        def rate_copy():
+            nc.vector.tensor_copy(out=rate_sb[:], in_=banks["rate"][:, 0 : 2 * G])
+
+        def cost_sum(c, n):
+            if ("cost", c // 2) not in banks:
+                banks["cost", c // 2] = new_bank(n)
+            rates = rate_sb[:].bitcast(BF16)
             for s in range(2):
+                col = 2 * (c % 2) + s
                 for k in range(4 * G):
-                    g, t = k // 4, k % 4
-                    u, e = t // 2, t % 2
+                    g, u, e = k // 4, k // 2 % 2, k % 2
                     mags = pos_abs[:, c, g, u].bitcast(BF16)
                     nc.tensor.matmul(
-                        out=cost_ps[c][:, s : s + 1],
+                        out=banks["cost", c // 2][:, col : col + 1],
                         lhsT=mags[:, 256 * s + e : 256 * s + 256 : 2],
-                        rhs=rate_sb[:, g, t : t + 1],
+                        rhs=rates[:, k : k + 1],
                         start=(k == 0),
                         stop=(k == 4 * G - 1),
                     )
 
-        def cost_spread_tensor(h, tag):
-            bank = psum.tile([P, 512], F32, name=tag, tag=tag, bufs=4)
+        def cost_column(h):
+            nc.vector.tensor_copy(out=cost_col[:, 4 * h : 4 * h + 4], in_=banks["cost", h][:, 0:4])
+
+        def cost_spread(h, n):
+            bank = new_bank(n)
             for m in range(4):
                 col = 4 * h + m
                 nc.tensor.transpose(bank[:, P * m : P * m + P], cost_col[:, col : col + 1].to_broadcast([P, P]), ident[:])
-            banks["cost", h] = bank
+            banks["spread", h] = bank
 
-        def cost_spread_copy(h):
-            nc.scalar.copy(out=cost_bc[:, 512 * h : 512 * h + 512], in_=banks["cost", h][:])
+        def cost_row(h):
+            nc.scalar.copy(out=cost_bc[:, 512 * h : 512 * h + 512], in_=banks["spread", h][:])
 
-        wide = {}
+        plain = {}
 
-        def new_wide(i):
-            if (i, 0) in wide:
-                return
-            wide[i, 0] = work.tile([P, K], BF16, name="wide_a", tag="wide_a", bufs=4, align_bytes=64)
-            wide[i, 1] = work.tile([P, K], BF16, name="wide_b", tag="wide_b", bufs=4, align_bytes=64)
+        def ret_block(i, s, b):
+            first = K * s + P * b
+            return ret_u8[i][:, first : first + P].bitcast(FP8)
 
-        def widen_a(i, first, last):
-            dst = wide[i, 0][:].rearrange("r (g u p e) -> r g p u e", g=G, u=2, e=2)
-            for b in range(first, last):
-                q = b % 4
-                if b // 4 >= GA[i]:
-                    nc.scalar.activation(
-                        out=wide[i, 0][:, P * b : P * b + P],
-                        in_=ret_u8[i][:, 0, P * b : P * b + P].bitcast(FP8),
-                        func=COPY,
-                        scale=scale_sb[:, 2 * i, b : b + 1],
+        def ret_halved(i, g):
+            if ("ret", i, g) not in halved:
+                halved["ret", i, g] = work.tile([P, 1024], BF16, name="ret_halved", tag="ret_halved", bufs=9, align_bytes=64)
+            return halved["ret", i, g]
+
+        def widen_vector(i, blocks, tiles=(0, 1)):
+            for b in blocks:
+                dst = ret_halved(i, b // 4)[:].rearrange("r (s u q w) -> r s q u w", s=2, u=2, w=16)
+                for s in tiles:
+                    nc.vector.tensor_scalar(
+                        out=dst[:, s, 4 * (b % 4) : 4 * (b % 4) + 4],
+                        in0=ret_block(i, s, b).rearrange("r (q u w) -> r q u w", u=2, w=16),
+                        scalar1=scale_sb[:, 2 * i + s, b : b + 1],
+                        scalar2=None,
+                        op0=ALU.mult,
                     )
-                    continue
-                nc.vector.tensor_scalar(
-                    out=dst[:, b // 4, 32 * q : 32 * q + 32],
-                    in0=ret_u8[i][:, 0, P * b : P * b + P].bitcast(FP8).rearrange("r (p u e) -> r p u e", u=2, e=2),
-                    scalar1=scale_sb[:, 2 * i, b : b + 1],
-                    scalar2=None,
-                    op0=ALU.mult,
-                )
 
-        def widen_b(i, first, last):
-            for b in range(first, last):
-                nc.scalar.activation(
-                    out=wide[i, 1][:, P * b : P * b + P],
-                    in_=ret_u8[i][:, 1, P * b : P * b + P].bitcast(FP8),
-                    func=COPY,
-                    scale=scale_sb[:, 2 * i + 1, b : b + 1],
-                )
+        def widen_scalar(i, blocks):
+            for b in blocks:
+                if (i, b // 4) not in plain:
+                    plain[i, b // 4] = work.tile([P, 1024], BF16, name="ret_plain", tag="ret_plain", bufs=4, align_bytes=64)
+                for s in range(2):
+                    first = 512 * s + P * (b % 4)
+                    nc.scalar.activation(
+                        out=plain[i, b // 4][:, first : first + P],
+                        in_=ret_block(i, s, b),
+                        func=COPY,
+                        scale=scale_sb[:, 2 * i + s, b : b + 1],
+                    )
 
-        def widen_b_v(i, first, last):
-            for b in range(first, last):
-                nc.vector.tensor_scalar(
-                    out=wide[i, 1][:, P * b : P * b + P],
-                    in0=ret_u8[i][:, 1, P * b : P * b + P].bitcast(FP8),
-                    scalar1=scale_sb[:, 2 * i + 1, b : b + 1],
-                    scalar2=None,
-                    op0=ALU.mult,
-                )
-
-        def permute_b(i):
-            perm[i] = work.tile([P, K], BF16, name="perm_b", tag="perm_b", bufs=3, align_bytes=64)
+        def ret_split(i, g, first=0):
             nc.scalar.copy(
-                out=perm[i][:].bitcast(F32).rearrange("r (g u p) -> r g u p", g=G, u=2),
-                in_=wide[i, 1][:].bitcast(F32).rearrange("r (g p u) -> r g u p", g=G, u=2),
+                out=ret_halved(i, g)[:].bitcast(F32).rearrange("r (s u q w) -> r s u q w", s=2, u=2, w=8)[:, :, :, 4 * first :],
+                in_=plain[i, g][:].bitcast(F32).rearrange("r (s q u w) -> r s u q w", s=2, u=2, w=8)[:, :, :, 4 * first :],
             )
-
-        perm = {}
-
-        def ret_transpose(i, g, tag="tp"):
-            words_a = wide[i, 0][:].bitcast(F32)
-            words_b = (perm[i] if i >= PERM_FROM else wide[i, 1])[:].bitcast(F32)
-            for g in (g,):
-                bank = psum.tile([P, 2, 256], F32, name=tag, tag=tag, bufs=4)
-                for u in range(2):
-                    a_cols = slice(256 * g + P * u, 256 * g + P * u + P) if g < GA[i] else slice(256 * g + u, 256 * g + 256, 2)
-                    nc.tensor.transpose(bank[:, u, 0:P], words_a[:, a_cols], ident[:])
-                for u in range(2):
-                    cols = slice(256 * g + P * u, 256 * g + P * u + P) if i >= PERM_FROM else slice(256 * g + u, 256 * g + 256, 2)
-                    nc.tensor.transpose(bank[:, u, P : 2 * P], words_b[:, cols], ident[:])
-                banks["ret", i, g] = bank
-
-        def ret_copy(i, g):
-            copy_out(("ret", i, g), "ret_grp", 6)
-
-        def ret_copy_v(i, g):
-            copy_out(("ret", i, g), "ret_grp", 6, nc.vector.tensor_copy)
 
         ret_q = {}
         ret_s = {}
 
-        def new_ret_q(i):
-            ret_q[i] = work.tile([P, G, 256], U32, name="ret_q", tag="ret_q", bufs=3, align_bytes=64)
-            ret_s[i] = work.tile([P, G, 256], U8, name="ret_s", tag="ret_s", bufs=3, align_bytes=64)
-
         def ret_quantize(i, g):
-            nc.vector.quantize_mx(
-                out=ret_q[i][:, g].bitcast(FP8X4),
-                scales=ret_s[i][:, g],
-                in_=grouped["ret", i, g][:].rearrange("p r t -> p (r t)"),
-            )
+            if g == 0:
+                ret_q[i] = work.tile([P, G, 256], U32, name="ret_q", tag="ret_q", bufs=4, align_bytes=64)
+                ret_s[i] = work.tile([P, G, 256], U8, name="ret_s", tag="ret_s", bufs=4, align_bytes=64)
+            nc.vector.quantize_mx(out=ret_q[i][:, g].bitcast(FP8X4), scales=ret_s[i][:, g], in_=grouped["ret", i, g][:])
 
         sums = {}
+        result = {}
 
-        def product(i, s, h, n0=0, n=512):
-            acc = psum.tile([P, n], F32, name="mx", tag="mx", bufs=4)
+        def product(tile, n0, bank, n=512):
+            i, s = tile // 2, tile % 2
+            acc = new_bank(bank)
             for g in range(G):
                 nc.tensor.matmul_mx(
-                    out=acc[:],
+                    out=acc[:, 0:n],
                     lhsT=ret_q[i][:, g, P * s : P * s + P].bitcast(FP8X4),
                     lhsT_scale=ret_s[i][:, g, P * s : P * s + P],
-                    rhs=pos_q[:, g, 512 * h + n0 : 512 * h + n0 + n].bitcast(FP8X4),
-                    rhs_scale=pos_s[:, g, 512 * h + n0 : 512 * h + n0 + n],
+                    rhs=pos_q[:, g, n0 : n0 + n].bitcast(FP8X4),
+                    rhs_scale=pos_s[:, g, n0 : n0 + n],
                     start=(g == 0),
                     stop=(g == G - 1),
                 )
-            sums[i, s, h, n0] = acc
+            sums[tile, n0] = acc
 
-        result = {}
+        def finish(tile, n0, n=512):
+            if tile not in result:
+                result[tile] = work.tile([P, N], F32, name="res", tag="res", bufs=6, align_bytes=64)
+            cols = slice(n0, n0 + n)
+            nc.vector.tensor_tensor(out=result[tile][:, cols], in0=sums[tile, n0][:, 0:n], in1=cost_bc[:, cols], op=ALU.subtract)
 
-        def finish(i, s, h, n0=0, n=512):
-            if h == 0:
-                result[i, s] = work.tile([P, N], F32, name="res", tag="res", bufs=6, align_bytes=64)
-            cols = slice(512 * h + n0, 512 * h + n0 + n)
-            nc.vector.tensor_tensor(out=result[i, s][:, cols], in0=sums[i, s, h, n0][:], in1=cost_bc[:, cols], op=ALU.subtract)
-            if i == PAIRS - 1 and s == 1:
-                nc.sync.dma_start(out=out_v[:, 2 * i + s, cols], in_=result[i, s][:, cols])
-            elif h == 1 and n0 + n == 512:
-                nc.sync.dma_start(out=out_v[:, 2 * i + s, :], in_=result[i, s][:])
+        def store(tile, n0=0, n=N):
+            nc.sync.dma_start(out=out_v[:, tile, n0 : n0 + n], in_=result[tile][:, n0 : n0 + n])
 
-        def pos_copies(c, nv):
+        def each_pass(step, *args):
             for g in range(G):
-                (pos_copy_v if g >= G - nv else pos_copy)(c, g)
+                step(*args, g)
 
-        def ret_copies(i, nv):
+        def copies(kind, pair, engines):
             for g in range(G):
-                (ret_copy_v if g >= G - nv else ret_copy)(i, g)
+                copy_out(kind, pair, g, engines[g])
 
-        def pos_codes(c):
-            for g in range(G):
-                pos_quantize(c, g)
+        vcopy = nc.vector.tensor_copy
+        scopy = nc.scalar.copy
 
-        def pos_magnitudes(c):
-            for g in range(G):
-                pos_absolute(c, g)
-
-        def widen_a12(i):
-            new_wide(i)
-            widen_a(i, 0, BLOCKS)
-
-        def widen_b12(i, nv):
-            new_wide(i)
-            widen_b(i, 0, BLOCKS - nv)
-            widen_b_v(i, BLOCKS - nv, BLOCKS)
-            if i >= PERM_FROM:
-                permute_b(i)
-
-        def ret_transposes(i, tag):
-            for g in range(G):
-                ret_transpose(i, g, tag)
-
-        def ret_codes(i):
-            new_ret_q(i)
-            for g in range(G):
-                ret_quantize(i, g)
-
-        def cost_column(c):
-            nc.vector.tensor_copy(out=cost_col[:, 2 * c : 2 * c + 2], in_=cost_ps[c][:])
-
+        nc.vector.memset(rate_rows[:], 0.0)
+        nc.scalar.dma_start(out=scale_sb[:], in_=ret_scale.rearrange("(p i) b -> p i b", i=TILES))
         load_ret(0)
-        load_pos(0, 0)
-        load_pos(0, 1)
-        load_pos(1, 0)
-        load_ret(1)
-        load_pos(1, 1)
-        load_pos(2, 0)
-        load_pos(2, 1)
-        load_pos(3, 0)
-        load_pos(3, 1)
-        load_ret(2)
-        load_ret(3)
-        load_ret(4)
-        load_ret(5)
-        load_ret(6)
-        load_ret(7)
-        widen_b12(0, 0)
-        pos_transpose(0, 0, "tp")
-        pos_transpose(0, 1, "mx")
-        widen_a12(0)
-        ret_transposes(0, "tp")
-        pos_copies(0, 1)
-        pos_magnitudes(0)
-        pos_transpose(1, 0, "mx")
-        pos_transpose(1, 1, "tp")
-        ret_copies(0, 0)
-        widen_a12(1)
-        ret_codes(0)
-        cost_sum(0, "tp")
-        pos_codes(0)
-        pos_transpose(2, 0, "tp")
-        pos_transpose(3, 0, "mx")
-        pos_transpose(2, 1, "tp")
-        pos_copies(1, 0)
-        pos_magnitudes(1)
-        widen_b12(1, 0)
-        pos_transpose(3, 1, "tp")
-        pos_codes(1)
-        pos_copies(3, 0)
-        cost_sum(1, "mx")
-        pos_copies(2, 1)
-        ret_transposes(1, "mx")
-        cost_column(0)
-        product(0, 0, 0)
-        ret_copies(1, 0)
-        product(0, 1, 0)
-        cost_column(1)
-        cost_spread_tensor(0, "tp")
-        pos_magnitudes(3)
-        cost_spread_copy(0)
-        pos_codes(2)
-        cost_sum(3, "tp")
-        pos_magnitudes(2)
-        ret_codes(1)
-        cost_sum(2, "tp")
-        product(1, 0, 0)
-        pos_codes(3)
-        product(1, 1, 0)
-        finish(0, 0, 0)
-        cost_column(3)
-        product(0, 0, 1)
-        finish(0, 1, 0)
-        widen_b12(2, 0)
-        cost_column(2)
-        product(1, 0, 1)
-        widen_b12(3, 0)
-        cost_spread_tensor(1, "tp")
-        widen_a12(2)
-        ret_transposes(2, "tp")
-        cost_spread_copy(1)
-        finish(1, 0, 0)
-        widen_a12(3)
-        ret_transposes(3, "tp")
-        finish(0, 0, 1)
-        finish(1, 1, 0)
-        ret_copies(2, 0)
-        finish(1, 0, 1)
-        product(1, 1, 1)
-        product(0, 1, 1)
-        ret_codes(2)
-        widen_b12(4, 0)
-        finish(1, 1, 1)
-        finish(0, 1, 1)
-        ret_copies(3, 0)
-        widen_a12(4)
+        for g in range(G):
+            nc.scalar.dma_start(out=rate_rows[2 * g : 2 * g + 2, :].rearrange("u (b w) -> u b w", w=16), in_=rate_v[g])
+        make_identity(nc, ident[:])
+        for m in range(POS_TILES):
+            load_pos(m)
+        for i in range(1, PAIRS):
+            load_ret(i)
+        on_scalar = (scopy, scopy, scopy)
 
-        for i in range(2, PAIRS):
-            far = i + 2
+        claim("ret", 0, (0, 1, 2))
+        claim("pos", 0, (3, 4, 5))
+        claim("pos", 1, (6, 0, 1))
+        claim("pos", 2, (2, 3, 4))
+        claim("pos", 3, (0, 1, 2))
+        claim("ret", 1, (4, 3, 1))
+        claim("ret", 2, (5, 6, 7))
+        widen_vector(0, range(0, 8))
+        widen_scalar(0, range(10, 12))
+        ret_split(0, 2, 2)
+        pos_split(0, vcopy)
+        widen_vector(0, range(8, 10))
+        pos_split(1, vcopy)
+        ret_turn(0, (0, 1))
+        pos_turn(0)
+        ret_turn(0, (2,))
+        pos_turn(1)
+        copies("ret", 0, on_scalar)
+        pos_split(2, vcopy)
+        pos_turn(2)
+        ret_quantize(0, 0)
+        ret_quantize(0, 1)
+        pos_split(3, vcopy)
+        copies("pos", 0, on_scalar)
+        pos_turn(3)
+        rate_turn(7)
+        ret_quantize(0, 2)
+        pos_quantize(0, 0)
+        pos_split(4, vcopy)
+        pos_turn(4)
+        rate_copy()
+        pos_quantize(0, 1)
+        pos_absolute(0, 0)
+        pos_split(5, vcopy)
+        pos_quantize(0, 2)
+        pos_absolute(0, 1)
+        pos_absolute(0, 2)
+        copies("pos", 1, on_scalar)
+        pos_turn(5)
+        cost_sum(0, 7)
+        each_pass(pos_quantize, 1)
+        copies("pos", 2, on_scalar)
+        product(0, 0, 5)
+        product(1, 0, 6)
+        pos_split(6, vcopy)
+        pos_split(7, vcopy)
+        each_pass(pos_absolute, 1)
+        pos_turn_pair(3)
+        cost_sum(1, 7)
+        widen_scalar(1, range(8, 12))
+        each_pass(pos_quantize, 2)
+        copy_out("pos", 3, 0, scopy)
+        ret_split(1, 2)
+        widen_vector(1, range(0, 8))
+        ret_turn(1, (0, 1))
+        cost_column(0)
+        copy_out("pos", 3, 1, scopy)
+        copy_out("pos", 3, 2, scopy)
+        each_pass(pos_absolute, 2)
+        cost_spread(0, 0)
+        ret_turn(1, (2,))
+        cost_row(0)
+        cost_sum(2, 7)
+        each_pass(pos_quantize, 3)
+        copies("ret", 1, on_scalar)
+        product(0, 512, 2)
+        each_pass(pos_absolute, 3)
+        cost_sum(3, 7)
+        product(1, 512, 0)
+        finish(0, 0)
+        widen_scalar(2, range(6, 12))
+        cost_column(1)
+        cost_spread(1, 3)
+        each_pass(ret_quantize, 1)
+        ret_split(2, 1, 2)
+        cost_row(1)
+        ret_split(2, 2)
+        finish(1, 0)
+        widen_vector(2, range(0, 6))
+        finish(0, 512)
+        store(0)
+
+        for i in range(1, PAIRS):
+            a, b = 2 * i, 2 * i + 1
+            product(a, 0, 4)
             if i + 1 < PAIRS:
-                ret_codes(i + 1)
-            for s in range(2):
-                for h in range(2):
-                    if i == PAIRS - 1 and s == 1 and h == 1:
-                        for n0 in (0, 256):
-                            product(i, s, h, n0, 256)
-                            finish(i, s, h, n0, 256)
-                    else:
-                        product(i, s, h)
-                        finish(i, s, h)
-            if far < PAIRS:
-                ret_transposes(far, "tp")
-                if far + 1 < PAIRS:
-                    new_wide(far + 1)
-                    widen_b(far + 1, 0, 8)
-                ret_copies(far, 0)
-                if far + 1 < PAIRS:
-                    widen_b(far + 1, 8, 12)
-                    if far + 1 >= PERM_FROM:
-                        permute_b(far + 1)
-                    widen_a(far + 1, 0, BLOCKS)
+                ret_turn(i + 1)
+            if i + 2 < PAIRS:
+                claim("ret", i + 2, (5, 6, 7))
+                widen_scalar(i + 2, range(6, 8))
+            if i + 1 < PAIRS:
+                copies("ret", i + 1, on_scalar)
+            finish(a - 1, 512)
+            store(a - 1)
+            if i + 2 < PAIRS:
+                widen_scalar(i + 2, range(8, 12))
+                ret_split(i + 2, 1, 2)
+                ret_split(i + 2, 2)
+                widen_vector(i + 2, range(0, 2))
+            finish(a, 0)
+            product(a, 512, 0)
+            if i + 1 < PAIRS:
+                each_pass(ret_quantize, i + 1)
+            product(b, 0, 1)
+            finish(a, 512)
+            store(a)
+            if i + 2 < PAIRS:
+                widen_vector(i + 2, range(2, 6))
+            if i + 1 < PAIRS:
+                product(b, 512, 2)
+                finish(b, 0)
+            else:
+                product(b, 512, 2, 256)
+                finish(b, 0)
+                store(b, 0, 512)
+                product(b, 768, 3, 256)
+                finish(b, 512, 256)
+                store(b, 512, 256)
+                finish(b, 768, 256)
+                store(b, 768, 256)

@@ -22,7 +22,6 @@ BLOCKS = K // 128
 TILES = T // P
 PAIRS = TILES // 2
 POS_TILES = N // P
-HALF_WORDS = K // 4
 
 
 def tile_scenario_profit_after_cost_d1_kernel(tc, ret_bytes, ret_scale, pos, rate, out):
@@ -34,8 +33,7 @@ def tile_scenario_profit_after_cost_d1_kernel(tc, ret_bytes, ret_scale, pos, rat
         ctx.enter_context(tc.manual_schedule())
 
         ident = const.tile([P, P], F32, name="ident")
-        rate_rows = const.tile([P, 2 * P], BF16, name="rate_rows")
-        rate_sb = const.tile([P, 2 * G], F32, name="rate_sb")
+        rate_sb = const.tile([P, G, 4], BF16, name="rate_sb")
         scale_sb = const.tile([P, TILES, BLOCKS], F32, name="scale_sb")
         pos_sb = [const.tile([P, K], BF16, name=f"pos_sb{m}", align_bytes=64) for m in range(POS_TILES)]
         ret_u8 = [const.tile([P, 2 * K], U8, name=f"ret_u8_{i}", align_bytes=64) for i in range(PAIRS)]
@@ -48,7 +46,6 @@ def tile_scenario_profit_after_cost_d1_kernel(tc, ret_bytes, ret_scale, pos, rat
         bytes_v = ret_bytes.rearrange("(p i s) k -> p i (s k)", i=PAIRS, s=2)
         out_v = out.rearrange("(p i) n -> p i n", i=TILES)
         pos_v = pos.rearrange("(m r) k -> m r k", r=P)
-        rate_v = rate.rearrange("(g b u w) -> g u b w", g=G, u=2, w=16)
 
         def new_bank(n):
             return psum.tile([P, 512], F32, name=f"bank{n}", tag=f"bank{n}")
@@ -59,36 +56,26 @@ def tile_scenario_profit_after_cost_d1_kernel(tc, ret_bytes, ret_scale, pos, rat
         def load_ret(i):
             nc.sync.dma_start(out=ret_u8[i][:], in_=bytes_v[:, i])
 
-        def split_halves(engine_copy, dst, src):
-            engine_copy(
-                out=dst.bitcast(F32).rearrange("r (u b w) -> r u b w", u=2, w=8),
-                in_=src.bitcast(F32).rearrange("r (b u w) -> r u b w", u=2, w=8),
-            )
-
         halved = {}
         banks = {}
         bank_of = {}
         grouped = {}
 
-        def pos_split(m, engine_copy):
-            halved["pos", m] = work.tile([P, K], BF16, name="pos_halved", tag="pos_halved", bufs=4, align_bytes=64)
-            split_halves(engine_copy, halved["pos", m][:], pos_sb[m][:])
-
         def claim(kind, pair, numbers):
             for g in range(G):
                 bank_of[kind, pair, g] = numbers[g]
 
-        def turn(kind, pair, g, s, words, plane):
+        def turn(kind, pair, g, s, planes):
             if (kind, pair, g) not in banks:
                 banks[kind, pair, g] = new_bank(bank_of[kind, pair, g])
             for u in range(2):
                 col = 256 * u + P * s
-                nc.tensor.transpose(banks[kind, pair, g][:, col : col + P], words[:, plane * u : plane * u + P], ident[:])
+                nc.tensor.transpose(banks[kind, pair, g][:, col : col + P], planes[u], ident[:])
 
         def pos_turn(m, passes=range(G)):
-            words = halved["pos", m][:].bitcast(F32)
+            words = pos_sb[m][:].bitcast(F32)
             for g in passes:
-                turn("pos", m // 2, g, m % 2, words[:, P * g :], HALF_WORDS)
+                turn("pos", m // 2, g, m % 2, [words[:, 256 * g + u : 256 * g + 256 : 2] for u in range(2)])
 
         def pos_turn_pair(c):
             for g in range(G):
@@ -99,7 +86,7 @@ def tile_scenario_profit_after_cost_d1_kernel(tc, ret_bytes, ret_scale, pos, rat
             for g in passes:
                 words = halved["ret", i, g][:].bitcast(F32)
                 for s in range(2):
-                    turn("ret", i, g, s, words[:, 256 * s :], P)
+                    turn("ret", i, g, s, [words[:, 256 * s + P * u : 256 * s + P * u + P] for u in range(2)])
 
         def copy_out(kind, pair, g, engine_copy):
             tile = work.tile([P, 1024], BF16, name="grouped", tag="grouped", bufs=8, align_bytes=64)
@@ -122,18 +109,10 @@ def tile_scenario_profit_after_cost_d1_kernel(tc, ret_bytes, ret_scale, pos, rat
                 op0=ALU.bitwise_and,
             )
 
-        def rate_turn(n):
-            bank = new_bank(n)
-            nc.tensor.transpose(bank[:, 0:P], rate_rows[:].bitcast(F32), ident[:])
-            banks["rate"] = bank
-
-        def rate_copy():
-            nc.vector.tensor_copy(out=rate_sb[:], in_=banks["rate"][:, 0 : 2 * G])
-
         def cost_sum(c, n):
             if ("cost", c // 2) not in banks:
                 banks["cost", c // 2] = new_bank(n)
-            rates = rate_sb[:].bitcast(BF16)
+            rates = rate_sb[:].rearrange("p g t -> p (g t)")
             for s in range(2):
                 col = 2 * (c % 2) + s
                 for k in range(4 * G):
@@ -173,11 +152,11 @@ def tile_scenario_profit_after_cost_d1_kernel(tc, ret_bytes, ret_scale, pos, rat
 
         def widen_vector(i, blocks, tiles=(0, 1)):
             for b in blocks:
-                dst = ret_halved(i, b // 4)[:].rearrange("r (s u q w) -> r s q u w", s=2, u=2, w=16)
+                dst = ret_halved(i, b // 4)[:].rearrange("r (s u p e) -> r s p u e", s=2, u=2, e=2)
                 for s in tiles:
                     nc.vector.tensor_scalar(
-                        out=dst[:, s, 4 * (b % 4) : 4 * (b % 4) + 4],
-                        in0=ret_block(i, s, b).rearrange("r (q u w) -> r q u w", u=2, w=16),
+                        out=dst[:, s, 32 * (b % 4) : 32 * (b % 4) + 32],
+                        in0=ret_block(i, s, b).rearrange("r (p u e) -> r p u e", u=2, e=2),
                         scalar1=scale_sb[:, 2 * i + s, b : b + 1],
                         scalar2=None,
                         op0=ALU.mult,
@@ -198,8 +177,8 @@ def tile_scenario_profit_after_cost_d1_kernel(tc, ret_bytes, ret_scale, pos, rat
 
         def ret_split(i, g, first=0):
             nc.scalar.copy(
-                out=ret_halved(i, g)[:].bitcast(F32).rearrange("r (s u q w) -> r s u q w", s=2, u=2, w=8)[:, :, :, 4 * first :],
-                in_=plain[i, g][:].bitcast(F32).rearrange("r (s q u w) -> r s u q w", s=2, u=2, w=8)[:, :, :, 4 * first :],
+                out=ret_halved(i, g)[:].bitcast(F32).rearrange("r (s u p) -> r s u p", s=2, u=2)[:, :, :, 32 * first :],
+                in_=plain[i, g][:].bitcast(F32).rearrange("r (s p u) -> r s u p", s=2, u=2)[:, :, :, 32 * first :],
             )
 
         ret_q = {}
@@ -249,11 +228,9 @@ def tile_scenario_profit_after_cost_d1_kernel(tc, ret_bytes, ret_scale, pos, rat
         vcopy = nc.vector.tensor_copy
         scopy = nc.scalar.copy
 
-        nc.vector.memset(rate_rows[:], 0.0)
         nc.scalar.dma_start(out=scale_sb[:], in_=ret_scale.rearrange("(p i) b -> p i b", i=TILES))
         load_ret(0)
-        for g in range(G):
-            nc.scalar.dma_start(out=rate_rows[2 * g : 2 * g + 2, :].rearrange("u (b w) -> u b w", w=16), in_=rate_v[g])
+        nc.scalar.dma_start(out=rate_sb[:], in_=rate.rearrange("(g p t) -> p g t", p=P, t=4))
         make_identity(nc, ident[:])
         for m in range(POS_TILES):
             load_pos(m)
@@ -271,30 +248,22 @@ def tile_scenario_profit_after_cost_d1_kernel(tc, ret_bytes, ret_scale, pos, rat
         widen_vector(0, range(0, 8))
         widen_scalar(0, range(10, 12))
         ret_split(0, 2, 2)
-        pos_split(0, vcopy)
         widen_vector(0, range(8, 10))
-        pos_split(1, vcopy)
         ret_turn(0, (0, 1))
         pos_turn(0)
         ret_turn(0, (2,))
         pos_turn(1)
         copies("ret", 0, on_scalar)
-        pos_split(2, vcopy)
         pos_turn(2)
         ret_quantize(0, 0)
         ret_quantize(0, 1)
-        pos_split(3, vcopy)
         copies("pos", 0, on_scalar)
         pos_turn(3)
-        rate_turn(7)
         ret_quantize(0, 2)
         pos_quantize(0, 0)
-        pos_split(4, vcopy)
         pos_turn(4)
-        rate_copy()
         pos_quantize(0, 1)
         pos_absolute(0, 0)
-        pos_split(5, vcopy)
         pos_quantize(0, 2)
         pos_absolute(0, 1)
         pos_absolute(0, 2)
@@ -305,8 +274,6 @@ def tile_scenario_profit_after_cost_d1_kernel(tc, ret_bytes, ret_scale, pos, rat
         copies("pos", 2, on_scalar)
         product(0, 0, 5)
         product(1, 0, 6)
-        pos_split(6, vcopy)
-        pos_split(7, vcopy)
         each_pass(pos_absolute, 1)
         pos_turn_pair(3)
         cost_sum(1, 7)

@@ -39,8 +39,10 @@ def tile_scenario_profit_after_cost_d1_kernel(tc, ret_bytes, ret_scale, pos, rat
         ret_u8 = [const.tile([P, 2 * K], U8, name=f"ret_u8_{i}", align_bytes=64) for i in range(PAIRS)]
         pos_q = const.tile([P, G, N], U32, name="pos_q", align_bytes=64)
         pos_s = const.tile([P, G, N], U8, name="pos_s", align_bytes=64)
-        pos_abs = const.tile([P, POS_TILES // 2, G, 2, 256], I32, name="pos_abs", align_bytes=64)
-        cost_col = const.tile([P, POS_TILES], F32, name="cost_col")
+        pos_abs = [
+            [const.tile([P, 2, 256], I32, name=f"pos_abs{c}_{g}", align_bytes=64) for g in range(G)] for c in range(POS_TILES // 2)
+        ]
+        cost_col = [const.tile([P, 4], F32, name=f"cost_col{h}") for h in range(2)]
         cost_bc = const.tile([P, N], F32, name="cost_bc", align_bytes=64)
 
         bytes_v = ret_bytes.rearrange("(p i s) k -> p i (s k)", i=PAIRS, s=2)
@@ -53,10 +55,11 @@ def tile_scenario_profit_after_cost_d1_kernel(tc, ret_bytes, ret_scale, pos, rat
         def load_pos(m):
             nc.sync.dma_start(out=pos_sb[m][:], in_=pos_v[m])
 
-        def load_ret(i):
-            nc.sync.dma_start(out=ret_u8[i][:], in_=bytes_v[:, i])
+        def load_ret(i, first=0, last=2):
+            nc.sync.dma_start(out=ret_u8[i][:, K * first : K * last], in_=bytes_v[:, i, K * first : K * last])
 
-        halved = {}
+        planes = {}
+        plain = {}
         banks = {}
         bank_of = {}
         grouped = {}
@@ -65,12 +68,12 @@ def tile_scenario_profit_after_cost_d1_kernel(tc, ret_bytes, ret_scale, pos, rat
             for g in range(G):
                 bank_of[kind, pair, g] = numbers[g]
 
-        def turn(kind, pair, g, s, planes):
+        def turn(kind, pair, g, s, halves):
             if (kind, pair, g) not in banks:
                 banks[kind, pair, g] = new_bank(bank_of[kind, pair, g])
             for u in range(2):
                 col = 256 * u + P * s
-                nc.tensor.transpose(banks[kind, pair, g][:, col : col + P], planes[u], ident[:])
+                nc.tensor.transpose(banks[kind, pair, g][:, col : col + P], halves[u], ident[:])
 
         def pos_turn(m, passes=range(G)):
             words = pos_sb[m][:].bitcast(F32)
@@ -82,11 +85,15 @@ def tile_scenario_profit_after_cost_d1_kernel(tc, ret_bytes, ret_scale, pos, rat
                 pos_turn(2 * c, (g,))
                 pos_turn(2 * c + 1, (g,))
 
-        def ret_turn(i, passes=range(G)):
+        def ret_turn(i, passes=range(G), tiles=(0, 1)):
             for g in passes:
-                words = halved["ret", i, g][:].bitcast(F32)
-                for s in range(2):
-                    turn("ret", i, g, s, [words[:, 256 * s + P * u : 256 * s + P * u + P] for u in range(2)])
+                for s in tiles:
+                    if (i, g, s) in planes:
+                        words = planes[i, g, s].bitcast(F32)
+                        turn("ret", i, g, s, [words[:, P * u : P * u + P] for u in range(2)])
+                    else:
+                        words = plain[i, g, s].bitcast(F32)
+                        turn("ret", i, g, s, [words[:, u::2] for u in range(2)])
 
         def copy_out(kind, pair, g, engine_copy):
             tile = work.tile([P, 1024], BF16, name="grouped", tag="grouped", bufs=8, align_bytes=64)
@@ -102,24 +109,24 @@ def tile_scenario_profit_after_cost_d1_kernel(tc, ret_bytes, ret_scale, pos, rat
 
         def pos_absolute(c, g):
             nc.vector.tensor_scalar(
-                out=pos_abs[:, c, g],
+                out=pos_abs[c][g][:],
                 in0=grouped["pos", c, g][:].bitcast(I32).rearrange("p (r u) -> p u r", u=2),
                 scalar1=0x7FFF7FFF,
                 scalar2=None,
                 op0=ALU.bitwise_and,
             )
 
-        def cost_sum(c, n):
-            if ("cost", c // 2) not in banks:
-                banks["cost", c // 2] = new_bank(n)
+        small = new_bank(7)
+
+        def cost_sum(c):
             rates = rate_sb[:].rearrange("p g t -> p (g t)")
             for s in range(2):
-                col = 2 * (c % 2) + s
+                col = 2 * c + s
                 for k in range(4 * G):
                     g, u, e = k // 4, k // 2 % 2, k % 2
-                    mags = pos_abs[:, c, g, u].bitcast(BF16)
+                    mags = pos_abs[c][g][:, u].bitcast(BF16)
                     nc.tensor.matmul(
-                        out=banks["cost", c // 2][:, col : col + 1],
+                        out=small[:, col : col + 1],
                         lhsT=mags[:, 256 * s + e : 256 * s + 256 : 2],
                         rhs=rates[:, k : k + 1],
                         start=(k == 0),
@@ -127,58 +134,59 @@ def tile_scenario_profit_after_cost_d1_kernel(tc, ret_bytes, ret_scale, pos, rat
                     )
 
         def cost_column(h):
-            nc.vector.tensor_copy(out=cost_col[:, 4 * h : 4 * h + 4], in_=banks["cost", h][:, 0:4])
+            nc.vector.tensor_copy(out=cost_col[h][:], in_=small[:, 4 * h : 4 * h + 4])
 
         def cost_spread(h, n):
             bank = new_bank(n)
             for m in range(4):
-                col = 4 * h + m
-                nc.tensor.transpose(bank[:, P * m : P * m + P], cost_col[:, col : col + 1].to_broadcast([P, P]), ident[:])
+                nc.tensor.transpose(bank[:, P * m : P * m + P], cost_col[h][:, m : m + 1].to_broadcast([P, P]), ident[:])
             banks["spread", h] = bank
 
         def cost_row(h):
             nc.scalar.copy(out=cost_bc[:, 512 * h : 512 * h + 512], in_=banks["spread", h][:])
 
-        plain = {}
-
         def ret_block(i, s, b):
             first = K * s + P * b
             return ret_u8[i][:, first : first + P].bitcast(FP8)
 
-        def ret_halved(i, g):
-            if ("ret", i, g) not in halved:
-                halved["ret", i, g] = work.tile([P, 1024], BF16, name="ret_halved", tag="ret_halved", bufs=9, align_bytes=64)
-            return halved["ret", i, g]
+        def rows_of(store, name, bufs, i, g, s):
+            if i == 0:
+                if (i, g, s) not in store:
+                    store[i, g, s] = const.tile([P, 512], BF16, name=f"first_{name}{g}_{s}", align_bytes=64)[:]
+            elif (i, g, s) not in store:
+                both = work.tile([P, 1024], BF16, name=name, tag=name, bufs=bufs, align_bytes=64)
+                store[i, g] = both[:]
+                store[i, g, 0] = both[:, 0:512]
+                store[i, g, 1] = both[:, 512:1024]
+            return store[i, g, s]
 
         def widen_vector(i, blocks, tiles=(0, 1)):
             for b in blocks:
-                dst = ret_halved(i, b // 4)[:].rearrange("r (s u p e) -> r s p u e", s=2, u=2, e=2)
                 for s in tiles:
+                    dst = rows_of(planes, "ret_planes", 9, i, b // 4, s).rearrange("r (u p e) -> r p u e", u=2, e=2)
                     nc.vector.tensor_scalar(
-                        out=dst[:, s, 32 * (b % 4) : 32 * (b % 4) + 32],
+                        out=dst[:, 32 * (b % 4) : 32 * (b % 4) + 32],
                         in0=ret_block(i, s, b).rearrange("r (p u e) -> r p u e", u=2, e=2),
                         scalar1=scale_sb[:, 2 * i + s, b : b + 1],
                         scalar2=None,
                         op0=ALU.mult,
                     )
 
-        def widen_scalar(i, blocks):
+        def widen_scalar(i, blocks, tiles=(0, 1)):
             for b in blocks:
-                if (i, b // 4) not in plain:
-                    plain[i, b // 4] = work.tile([P, 1024], BF16, name="ret_plain", tag="ret_plain", bufs=4, align_bytes=64)
-                for s in range(2):
-                    first = 512 * s + P * (b % 4)
+                for s in tiles:
                     nc.scalar.activation(
-                        out=plain[i, b // 4][:, first : first + P],
+                        out=rows_of(plain, "ret_plain", 4, i, b // 4, s)[:, P * (b % 4) : P * (b % 4) + P],
                         in_=ret_block(i, s, b),
                         func=COPY,
                         scale=scale_sb[:, 2 * i + s, b : b + 1],
                     )
 
         def ret_split(i, g, first=0):
+            rows_of(planes, "ret_planes", 9, i, g, 0)
             nc.scalar.copy(
-                out=ret_halved(i, g)[:].bitcast(F32).rearrange("r (s u p) -> r s u p", s=2, u=2)[:, :, :, 32 * first :],
-                in_=plain[i, g][:].bitcast(F32).rearrange("r (s p u) -> r s u p", s=2, u=2)[:, :, :, 32 * first :],
+                out=planes[i, g].bitcast(F32).rearrange("r (s u p) -> r s u p", s=2, u=2)[:, :, :, 32 * first :],
+                in_=plain[i, g].bitcast(F32).rearrange("r (s p u) -> r s u p", s=2, u=2)[:, :, :, 32 * first :],
             )
 
         ret_q = {}
@@ -229,7 +237,8 @@ def tile_scenario_profit_after_cost_d1_kernel(tc, ret_bytes, ret_scale, pos, rat
         scopy = nc.scalar.copy
 
         nc.scalar.dma_start(out=scale_sb[:], in_=ret_scale.rearrange("(p i) b -> p i b", i=TILES))
-        load_ret(0)
+        load_ret(0, 0, 1)
+        load_ret(0, 1, 2)
         nc.scalar.dma_start(out=rate_sb[:], in_=rate.rearrange("(g p t) -> p g t", p=P, t=4))
         make_identity(nc, ident[:])
         for m in range(POS_TILES):
@@ -242,108 +251,104 @@ def tile_scenario_profit_after_cost_d1_kernel(tc, ret_bytes, ret_scale, pos, rat
         claim("pos", 0, (3, 4, 5))
         claim("pos", 1, (6, 0, 1))
         claim("pos", 2, (2, 3, 4))
-        claim("pos", 3, (0, 1, 2))
-        claim("ret", 1, (4, 3, 1))
-        claim("ret", 2, (5, 6, 7))
-        widen_vector(0, range(0, 8))
-        widen_scalar(0, range(10, 12))
-        ret_split(0, 2, 2)
-        widen_vector(0, range(8, 10))
-        ret_turn(0, (0, 1))
-        pos_turn(0)
-        ret_turn(0, (2,))
-        pos_turn(1)
-        copies("ret", 0, on_scalar)
-        pos_turn(2)
-        ret_quantize(0, 0)
-        ret_quantize(0, 1)
-        copies("pos", 0, on_scalar)
-        pos_turn(3)
-        ret_quantize(0, 2)
-        pos_quantize(0, 0)
-        pos_turn(4)
-        pos_quantize(0, 1)
-        pos_absolute(0, 0)
-        pos_quantize(0, 2)
-        pos_absolute(0, 1)
-        pos_absolute(0, 2)
-        copies("pos", 1, on_scalar)
-        pos_turn(5)
-        cost_sum(0, 7)
-        each_pass(pos_quantize, 1)
-        copies("pos", 2, on_scalar)
-        product(0, 0, 5)
-        product(1, 0, 6)
-        each_pass(pos_absolute, 1)
-        pos_turn_pair(3)
-        cost_sum(1, 7)
-        widen_scalar(1, range(8, 12))
-        each_pass(pos_quantize, 2)
-        copy_out("pos", 3, 0, scopy)
-        ret_split(1, 2)
-        widen_vector(1, range(0, 8))
-        ret_turn(1, (0, 1))
+        claim("pos", 3, (5, 6, 0))
+        claim("ret", 1, (3, 4, 5))
+        claim("ret", 2, (1, 2, 7))
+        for s in range(2):
+            widen_vector(0, range(0, 8), (s,))
+            widen_scalar(0, range(8, 12), (s,))
+            ret_turn(0, tiles=(s,))
+        copies("ret", 0, (scopy, vcopy, scopy))
+        each_pass(ret_quantize, 0)
+        for c in range(4):
+            pos_turn(2 * c)
+            pos_turn(2 * c + 1)
+            copies("pos", c, on_scalar)
+            if c < 3:
+                each_pass(pos_quantize, c)
+                each_pass(pos_absolute, c)
+        widen_vector(1, range(0, 10))
+        widen_scalar(1, range(10, 12))
+        ret_split(1, 2, 2)
+        product(0, 0, 1)
+        cost_sum(0)
+        cost_sum(1)
+        product(1, 0, 2)
         cost_column(0)
-        copy_out("pos", 3, 1, scopy)
-        copy_out("pos", 3, 2, scopy)
-        each_pass(pos_absolute, 2)
-        cost_spread(0, 0)
-        ret_turn(1, (2,))
-        cost_row(0)
-        cost_sum(2, 7)
         each_pass(pos_quantize, 3)
-        copies("ret", 1, on_scalar)
-        product(0, 512, 2)
         each_pass(pos_absolute, 3)
-        cost_sum(3, 7)
-        product(1, 512, 0)
+        ret_turn(1)
+        cost_spread(0, 6)
+        cost_sum(2)
+        widen_scalar(2, range(6, 8))
+        copy_out("ret", 1, 0, scopy)
+        cost_row(0)
+        copy_out("ret", 1, 1, scopy)
+        copy_out("ret", 1, 2, scopy)
+        product(0, 512, 0)
+        cost_sum(3)
+        widen_vector(2, range(0, 3))
         finish(0, 0)
-        widen_scalar(2, range(6, 12))
         cost_column(1)
-        cost_spread(1, 3)
+        product(1, 512, 6)
         each_pass(ret_quantize, 1)
+        cost_spread(1, 4)
+        widen_scalar(2, range(8, 12))
         ret_split(2, 1, 2)
         cost_row(1)
         ret_split(2, 2)
         finish(1, 0)
-        widen_vector(2, range(0, 6))
+        widen_vector(2, range(3, 6))
         finish(0, 512)
         store(0)
 
+        sum_banks = (3, 5, 0, 6, 4)
         for i in range(1, PAIRS):
             a, b = 2 * i, 2 * i + 1
-            product(a, 0, 4)
-            if i + 1 < PAIRS:
+            last = i + 1 == PAIRS
+            bank = [sum_banks[(4 * (i - 1) + j) % len(sum_banks)] for j in range(5)]
+            product(a, 0, bank[0])
+            if not last:
                 ret_turn(i + 1)
             if i + 2 < PAIRS:
-                claim("ret", i + 2, (5, 6, 7))
+                claim("ret", i + 2, (1, 2, 7))
                 widen_scalar(i + 2, range(6, 8))
-            if i + 1 < PAIRS:
+            if not last:
                 copies("ret", i + 1, on_scalar)
             finish(a - 1, 512)
-            store(a - 1)
+            if last:
+                store(a - 1, 512, 512)
+            else:
+                store(a - 1)
             if i + 2 < PAIRS:
                 widen_scalar(i + 2, range(8, 12))
                 ret_split(i + 2, 1, 2)
                 ret_split(i + 2, 2)
                 widen_vector(i + 2, range(0, 2))
             finish(a, 0)
-            product(a, 512, 0)
-            if i + 1 < PAIRS:
+            if last:
+                store(a, 0, 512)
+            product(a, 512, bank[1])
+            if not last:
                 each_pass(ret_quantize, i + 1)
-            product(b, 0, 1)
+            product(b, 0, bank[2])
             finish(a, 512)
-            store(a)
+            if last:
+                store(a, 512, 512)
+            else:
+                store(a)
             if i + 2 < PAIRS:
                 widen_vector(i + 2, range(2, 6))
-            if i + 1 < PAIRS:
-                product(b, 512, 2)
+            if not last:
+                product(b, 512, bank[3])
                 finish(b, 0)
+                if i + 2 == PAIRS:
+                    store(b, 0, 512)
             else:
-                product(b, 512, 2, 256)
+                product(b, 512, bank[3], 256)
                 finish(b, 0)
                 store(b, 0, 512)
-                product(b, 768, 3, 256)
+                product(b, 768, bank[4], 256)
                 finish(b, 512, 256)
                 store(b, 512, 256)
                 finish(b, 768, 256)

@@ -218,7 +218,7 @@ def tile_scenario_profit_after_cost_d1_kernel(tc, ret_bytes, ret_scale, pos, rat
 
         def finish(tile, n0, n=512):
             if tile not in result:
-                result[tile] = work.tile([P, N], F32, name="res", tag="res", bufs=6, align_bytes=64)
+                result[tile] = const.tile([P, N], F32, name=f"result{tile}", align_bytes=64)
             cols = slice(n0, n0 + n)
             nc.vector.tensor_tensor(out=result[tile][:, cols], in0=sums[tile, n0][:, 0:n], in1=cost_bc[:, cols], op=ALU.subtract)
 

@@ -96,7 +96,7 @@ def tile_scenario_profit_after_cost_d1_kernel(tc, ret_bytes, ret_scale, pos, rat
                         turn("ret", i, g, s, [words[:, u::2] for u in range(2)])
 
         def copy_out(kind, pair, g, engine_copy):
-            tile = work.tile([P, 1024], BF16, name="grouped", tag="grouped", bufs=8, align_bytes=64)
+            tile = work.tile([P, 1024], BF16, name="grouped", tag="grouped", bufs=12, align_bytes=64)
             engine_copy(
                 out=tile[:].bitcast(F32).rearrange("p (r u) -> p r u", u=2),
                 in_=banks[kind, pair, g][:].rearrange("p (u r) -> p r u", u=2),
@@ -126,15 +126,15 @@ def tile_scenario_profit_after_cost_d1_kernel(tc, ret_bytes, ret_scale, pos, rat
                     g, u, e = k // 4, k // 2 % 2, k % 2
                     mags = pos_abs[c][g][:, u].bitcast(BF16)
                     nc.tensor.matmul(
-                        out=small[:, col : col + 1],
+                        out=small[:, 48 * col : 48 * col + 48],
                         lhsT=mags[:, 256 * s + e : 256 * s + 256 : 2],
-                        rhs=rates[:, k : k + 1],
+                        rhs=rates[:, k : k + 1].to_broadcast([P, 48]),
                         start=(k == 0),
                         stop=(k == 4 * G - 1),
                     )
 
         def cost_column(h):
-            nc.vector.tensor_copy(out=cost_col[h][:], in_=small[:, 4 * h : 4 * h + 4])
+            nc.vector.tensor_copy(out=cost_col[h][:], in_=small[:, 192 * h : 192 * h + 192 : 48])
 
         def cost_spread(h, n):
             bank = new_bank(n)
@@ -267,12 +267,13 @@ def tile_scenario_profit_after_cost_d1_kernel(tc, ret_bytes, ret_scale, pos, rat
             if c < 3:
                 each_pass(pos_quantize, c)
                 each_pass(pos_absolute, c)
-        widen_vector(1, range(0, 10))
+        widen_vector(1, (8, 9))
+        widen_vector(1, range(0, 8))
         widen_scalar(1, range(10, 12))
         ret_split(1, 2, 2)
-        product(0, 0, 1)
         cost_sum(0)
         cost_sum(1)
+        product(0, 0, 1)
         product(1, 0, 2)
         cost_column(0)
         each_pass(pos_quantize, 3)
@@ -287,8 +288,9 @@ def tile_scenario_profit_after_cost_d1_kernel(tc, ret_bytes, ret_scale, pos, rat
         copy_out("ret", 1, 2, scopy)
         product(0, 512, 0)
         cost_sum(3)
-        widen_vector(2, range(0, 3))
+        widen_vector(2, (4, 5, 0))
         finish(0, 0)
+        widen_vector(2, range(1, 4))
         cost_column(1)
         product(1, 512, 6)
         each_pass(ret_quantize, 1)
@@ -298,7 +300,6 @@ def tile_scenario_profit_after_cost_d1_kernel(tc, ret_bytes, ret_scale, pos, rat
         cost_row(1)
         ret_split(2, 2)
         finish(1, 0)
-        widen_vector(2, range(3, 6))
         finish(0, 512)
         store(0)
 
@@ -324,7 +325,7 @@ def tile_scenario_profit_after_cost_d1_kernel(tc, ret_bytes, ret_scale, pos, rat
                 widen_scalar(i + 2, range(8, 12))
                 ret_split(i + 2, 1, 2)
                 ret_split(i + 2, 2)
-                widen_vector(i + 2, range(0, 2))
+                widen_vector(i + 2, range(4, 6))
             finish(a, 0)
             if last:
                 store(a, 0, 512)
@@ -338,7 +339,7 @@ def tile_scenario_profit_after_cost_d1_kernel(tc, ret_bytes, ret_scale, pos, rat
             else:
                 store(a)
             if i + 2 < PAIRS:
-                widen_vector(i + 2, range(2, 6))
+                widen_vector(i + 2, range(0, 4))
             if not last:
                 product(b, 512, bank[3])
                 finish(b, 0)

@@ -313,7 +313,8 @@ def tile_scenario_profit_after_cost_d1_kernel(tc, ret_bytes, ret_scale, pos, rat
                 ret_turn(i + 1)
             if i + 2 < PAIRS:
                 claim("ret", i + 2, (1, 2, 7))
-                widen_scalar(i + 2, range(6, 8))
+                widen_vector(i + 2, range(0, 7))
+                widen_scalar(i + 2, range(7, 9))
             if not last:
                 copies("ret", i + 1, on_scalar)
             finish(a - 1, 512)
@@ -322,10 +323,9 @@ def tile_scenario_profit_after_cost_d1_kernel(tc, ret_bytes, ret_scale, pos, rat
             else:
                 store(a - 1)
             if i + 2 < PAIRS:
-                widen_scalar(i + 2, range(8, 12))
-                ret_split(i + 2, 1, 2)
+                widen_scalar(i + 2, range(9, 12))
+                ret_split(i + 2, 1, 3)
                 ret_split(i + 2, 2)
-                widen_vector(i + 2, range(4, 6))
             finish(a, 0)
             if last:
                 store(a, 0, 512)
@@ -338,8 +338,6 @@ def tile_scenario_profit_after_cost_d1_kernel(tc, ret_bytes, ret_scale, pos, rat
                 store(a, 512, 512)
             else:
                 store(a)
-            if i + 2 < PAIRS:
-                widen_vector(i + 2, range(0, 4))
             if not last:
                 product(b, 512, bank[3])
                 finish(b, 0)

@@ -261,6 +261,8 @@ def tile_scenario_profit_after_cost_d1_kernel(tc, ret_bytes, ret_scale, pos, rat
         copies("ret", 0, (scopy, vcopy, scopy))
         each_pass(ret_quantize, 0)
         for c in range(4):
+            if c == 3:
+                cost_sum(0)
             pos_turn(2 * c)
             pos_turn(2 * c + 1)
             copies("pos", c, on_scalar)
@@ -271,7 +273,6 @@ def tile_scenario_profit_after_cost_d1_kernel(tc, ret_bytes, ret_scale, pos, rat
         widen_vector(1, range(0, 8))
         widen_scalar(1, range(10, 12))
         ret_split(1, 2, 2)
-        cost_sum(0)
         cost_sum(1)
         product(0, 0, 1)
         product(1, 0, 2)

@@ -109,8 +109,8 @@ def tile_scenario_profit_after_cost_d1_kernel(tc, ret_bytes, ret_scale, pos, rat
 
         def pos_absolute(c, g):
             nc.vector.tensor_scalar(
-                out=pos_abs[c][g][:],
-                in0=grouped["pos", c, g][:].bitcast(I32).rearrange("p (r u) -> p u r", u=2),
+                out=pos_abs[c][g][:].rearrange("p u r -> p r u"),
+                in0=grouped["pos", c, g][:].bitcast(I32).rearrange("p (r u) -> p r u", u=2),
                 scalar1=0x7FFF7FFF,
                 scalar2=None,
                 op0=ALU.bitwise_and,
@@ -266,7 +266,7 @@ def tile_scenario_profit_after_cost_d1_kernel(tc, ret_bytes, ret_scale, pos, rat
             pos_turn(2 * c)
             pos_turn(2 * c + 1)
             copies("pos", c, on_scalar)
-            if c < 3:
+            if c < 2:
                 each_pass(pos_quantize, c)
                 each_pass(pos_absolute, c)
         widen_vector(1, (8, 9))
@@ -277,6 +277,8 @@ def tile_scenario_profit_after_cost_d1_kernel(tc, ret_bytes, ret_scale, pos, rat
         product(0, 0, 1)
         product(1, 0, 2)
         cost_column(0)
+        each_pass(pos_quantize, 2)
+        each_pass(pos_absolute, 2)
         each_pass(pos_quantize, 3)
         each_pass(pos_absolute, 3)
         ret_turn(1)

@@ -34,7 +34,9 @@ def tile_scenario_profit_after_cost_d1_kernel(tc, ret_bytes, ret_scale, pos, rat
 
         ident = const.tile([P, P], F32, name="ident")
         rate_sb = const.tile([P, G, 4], BF16, name="rate_sb")
-        scale_sb = const.tile([P, TILES, BLOCKS], F32, name="scale_sb")
+        scale_first = const.tile([P, 2, BLOCKS], F32, name="scale_first")
+        scale_rest = const.tile([P, TILES - 2, BLOCKS], F32, name="scale_rest")
+        first_pass = const.tile([P, 512], U8, name="first_pass", align_bytes=64)
         pos_sb = [const.tile([P, K], BF16, name=f"pos_sb{m}", align_bytes=64) for m in range(POS_TILES)]
         ret_u8 = [const.tile([P, 2 * K], U8, name=f"ret_u8_{i}", align_bytes=64) for i in range(PAIRS)]
         pos_q = const.tile([P, G, N], U32, name="pos_q", align_bytes=64)
@@ -55,8 +57,8 @@ def tile_scenario_profit_after_cost_d1_kernel(tc, ret_bytes, ret_scale, pos, rat
         def load_pos(m):
             nc.sync.dma_start(out=pos_sb[m][:], in_=pos_v[m])
 
-        def load_ret(i, first=0, last=2):
-            nc.sync.dma_start(out=ret_u8[i][:, K * first : K * last], in_=bytes_v[:, i, K * first : K * last])
+        def load_ret(i, first=0, last=2 * K):
+            nc.sync.dma_start(out=ret_u8[i][:, first:last], in_=bytes_v[:, i, first:last])
 
         planes = {}
         plain = {}
@@ -118,7 +120,7 @@ def tile_scenario_profit_after_cost_d1_kernel(tc, ret_bytes, ret_scale, pos, rat
 
         small = new_bank(7)
 
-        def cost_sum(c):
+        def cost_sum(c, width):
             rates = rate_sb[:].rearrange("p g t -> p (g t)")
             for s in range(2):
                 col = 2 * c + s
@@ -126,9 +128,9 @@ def tile_scenario_profit_after_cost_d1_kernel(tc, ret_bytes, ret_scale, pos, rat
                     g, u, e = k // 4, k // 2 % 2, k % 2
                     mags = pos_abs[c][g][:, u].bitcast(BF16)
                     nc.tensor.matmul(
-                        out=small[:, 48 * col : 48 * col + 48],
+                        out=small[:, 48 * col : 48 * col + width],
                         lhsT=mags[:, 256 * s + e : 256 * s + 256 : 2],
-                        rhs=rates[:, k : k + 1].to_broadcast([P, 48]),
+                        rhs=rates[:, k : k + 1].to_broadcast([P, width]),
                         start=(k == 0),
                         stop=(k == 4 * G - 1),
                     )
@@ -145,8 +147,15 @@ def tile_scenario_profit_after_cost_d1_kernel(tc, ret_bytes, ret_scale, pos, rat
         def cost_row(h):
             nc.scalar.copy(out=cost_bc[:, 512 * h : 512 * h + 512], in_=banks["spread", h][:])
 
+        def scale_of(i, s, b):
+            if i == 0:
+                return scale_first[:, s, b : b + 1]
+            return scale_rest[:, 2 * i + s - 2, b : b + 1]
+
         def ret_block(i, s, b):
             first = K * s + P * b
+            if i == 0 and first < 512:
+                return first_pass[:, first : first + P].bitcast(FP8)
             return ret_u8[i][:, first : first + P].bitcast(FP8)
 
         def rows_of(store, name, bufs, i, g, s):
@@ -167,7 +176,18 @@ def tile_scenario_profit_after_cost_d1_kernel(tc, ret_bytes, ret_scale, pos, rat
                     nc.vector.tensor_scalar(
                         out=dst[:, 32 * (b % 4) : 32 * (b % 4) + 32],
                         in0=ret_block(i, s, b).rearrange("r (p u e) -> r p u e", u=2, e=2),
-                        scalar1=scale_sb[:, 2 * i + s, b : b + 1],
+                        scalar1=scale_of(i, s, b),
+                        scalar2=None,
+                        op0=ALU.mult,
+                    )
+
+        def widen_vector_plain(i, blocks, tiles=(0, 1)):
+            for b in blocks:
+                for s in tiles:
+                    nc.vector.tensor_scalar(
+                        out=rows_of(plain, "ret_plain", 4, i, b // 4, s)[:, P * (b % 4) : P * (b % 4) + P],
+                        in0=ret_block(i, s, b),
+                        scalar1=scale_of(i, s, b),
                         scalar2=None,
                         op0=ALU.mult,
                     )
@@ -179,7 +199,7 @@ def tile_scenario_profit_after_cost_d1_kernel(tc, ret_bytes, ret_scale, pos, rat
                         out=rows_of(plain, "ret_plain", 4, i, b // 4, s)[:, P * (b % 4) : P * (b % 4) + P],
                         in_=ret_block(i, s, b),
                         func=COPY,
-                        scale=scale_sb[:, 2 * i + s, b : b + 1],
+                        scale=scale_of(i, s, b),
                     )
 
         def ret_split(i, g, first=0):
@@ -236,12 +256,16 @@ def tile_scenario_profit_after_cost_d1_kernel(tc, ret_bytes, ret_scale, pos, rat
         vcopy = nc.vector.tensor_copy
         scopy = nc.scalar.copy
 
-        nc.scalar.dma_start(out=scale_sb[:], in_=ret_scale.rearrange("(p i) b -> p i b", i=TILES))
-        load_ret(0, 0, 1)
-        load_ret(0, 1, 2)
+        scale_v = ret_scale.rearrange("(p i) b -> p i b", i=TILES)
+        nc.scalar.dma_start(out=scale_first[:], in_=scale_v[:, 0:2])
+        nc.sync.dma_start(out=first_pass[:], in_=bytes_v[:, 0, 0:512])
+        load_ret(0, 512, K)
+        load_ret(0, K, 2 * K)
         nc.scalar.dma_start(out=rate_sb[:], in_=rate.rearrange("(g p t) -> p g t", p=P, t=4))
         make_identity(nc, ident[:])
         for m in range(POS_TILES):
+            if m == 7:
+                nc.sync.dma_start(out=scale_rest[:], in_=scale_v[:, 2:TILES])
             load_pos(m)
         for i in range(1, PAIRS):
             load_ret(i)
@@ -254,26 +278,30 @@ def tile_scenario_profit_after_cost_d1_kernel(tc, ret_bytes, ret_scale, pos, rat
         claim("pos", 3, (5, 6, 0))
         claim("ret", 1, (3, 4, 5))
         claim("ret", 2, (1, 2, 7))
-        for s in range(2):
-            widen_vector(0, range(0, 8), (s,))
-            widen_scalar(0, range(8, 12), (s,))
-            ret_turn(0, tiles=(s,))
+        widen_scalar(0, range(8, 12), (0,))
+        widen_vector(0, range(0, 8), (0,))
+        widen_vector(0, range(0, 12), (1,))
+        ret_turn(0, (0, 1), (0,))
+        ret_turn(0, range(G), (1,))
+        pos_turn(0)
+        ret_turn(0, (2,), (0,))
         copies("ret", 0, (scopy, vcopy, scopy))
         each_pass(ret_quantize, 0)
-        for c in range(4):
-            if c == 3:
-                cost_sum(0)
-            pos_turn(2 * c)
-            pos_turn(2 * c + 1)
-            copies("pos", c, on_scalar)
-            if c < 2:
-                each_pass(pos_quantize, c)
-                each_pass(pos_absolute, c)
+        for m in range(1, POS_TILES):
+            c = m // 2
+            if m == 6:
+                cost_sum(0, 48)
+            pos_turn(m)
+            if m % 2 == 1:
+                copies("pos", c, on_scalar)
+                if c < 2:
+                    each_pass(pos_absolute, c)
+                    each_pass(pos_quantize, c)
         widen_vector(1, (8, 9))
         widen_vector(1, range(0, 8))
         widen_scalar(1, range(10, 12))
         ret_split(1, 2, 2)
-        cost_sum(1)
+        cost_sum(1, 48)
         product(0, 0, 1)
         product(1, 0, 2)
         cost_column(0)
@@ -283,14 +311,14 @@ def tile_scenario_profit_after_cost_d1_kernel(tc, ret_bytes, ret_scale, pos, rat
         each_pass(pos_absolute, 3)
         ret_turn(1)
         cost_spread(0, 6)
-        cost_sum(2)
+        cost_sum(2, 48)
         widen_scalar(2, range(6, 8))
         copy_out("ret", 1, 0, scopy)
         cost_row(0)
         copy_out("ret", 1, 1, scopy)
         copy_out("ret", 1, 2, scopy)
         product(0, 512, 0)
-        cost_sum(3)
+        cost_sum(3, 48)
         widen_vector(2, (4, 5, 0))
         finish(0, 0)
         widen_vector(2, range(1, 4))
@@ -314,10 +342,11 @@ def tile_scenario_profit_after_cost_d1_kernel(tc, ret_bytes, ret_scale, pos, rat
             product(a, 0, bank[0])
             if not last:
                 ret_turn(i + 1)
+            share = 7 - i % 2
             if i + 2 < PAIRS:
                 claim("ret", i + 2, (1, 2, 7))
-                widen_vector(i + 2, range(0, 7))
-                widen_scalar(i + 2, range(7, 9))
+                widen_vector(i + 2, range(0, share))
+                widen_scalar(i + 2, range(share, share + 2))
             if not last:
                 copies("ret", i + 1, on_scalar)
             finish(a - 1, 512)
@@ -326,8 +355,8 @@ def tile_scenario_profit_after_cost_d1_kernel(tc, ret_bytes, ret_scale, pos, rat
             else:
                 store(a - 1)
             if i + 2 < PAIRS:
-                widen_scalar(i + 2, range(9, 12))
-                ret_split(i + 2, 1, 3)
+                widen_scalar(i + 2, range(share + 2, 12))
+                ret_split(i + 2, 1, share - 4)
                 ret_split(i + 2, 2)
             finish(a, 0)
             if last:

@@ -277,19 +277,18 @@ def tile_scenario_profit_after_cost_d1_kernel(tc, ret_bytes, ret_scale, pos, rat
         claim("pos", 2, (2, 3, 4))
         claim("pos", 3, (5, 6, 0))
         claim("ret", 1, (3, 4, 5))
-        claim("ret", 2, (1, 2, 7))
         widen_scalar(0, range(8, 12), (0,))
         widen_vector(0, range(0, 8), (0,))
         widen_vector(0, range(0, 12), (1,))
         ret_turn(0, (0, 1), (0,))
-        ret_turn(0, range(G), (1,))
+        ret_turn(0, (0, 1), (1,))
         pos_turn(0)
-        ret_turn(0, (2,), (0,))
+        ret_turn(0, (2,), (1, 0))
         copies("ret", 0, (scopy, vcopy, scopy))
         each_pass(ret_quantize, 0)
         for m in range(1, POS_TILES):
             c = m // 2
-            if m == 6:
+            if m == 7:
                 cost_sum(0, 48)
             pos_turn(m)
             if m % 2 == 1:
@@ -319,68 +318,96 @@ def tile_scenario_profit_after_cost_d1_kernel(tc, ret_bytes, ret_scale, pos, rat
         copy_out("ret", 1, 2, scopy)
         product(0, 512, 0)
         cost_sum(3, 48)
-        widen_vector(2, (4, 5, 0))
         finish(0, 0)
-        widen_vector(2, range(1, 4))
+        widen_vector(2, range(0, 3))
         cost_column(1)
         product(1, 512, 6)
         each_pass(ret_quantize, 1)
         cost_spread(1, 4)
+        widen_vector(2, range(3, 6))
         widen_scalar(2, range(8, 12))
         ret_split(2, 1, 2)
         cost_row(1)
         ret_split(2, 2)
         finish(1, 0)
-        finish(0, 512)
-        store(0)
 
-        sum_banks = (3, 5, 0, 6, 4)
-        for i in range(1, PAIRS):
-            a, b = 2 * i, 2 * i + 1
-            last = i + 1 == PAIRS
-            bank = [sum_banks[(4 * (i - 1) + j) % len(sum_banks)] for j in range(5)]
-            product(a, 0, bank[0])
-            if not last:
-                ret_turn(i + 1)
-            share = 7 - i % 2
-            if i + 2 < PAIRS:
-                claim("ret", i + 2, (1, 2, 7))
-                widen_vector(i + 2, range(0, share))
-                widen_scalar(i + 2, range(share, share + 2))
-            if not last:
-                copies("ret", i + 1, on_scalar)
-            finish(a - 1, 512)
-            if last:
-                store(a - 1, 512, 512)
-            else:
-                store(a - 1)
-            if i + 2 < PAIRS:
-                widen_scalar(i + 2, range(share + 2, 12))
-                ret_split(i + 2, 1, share - 4)
-                ret_split(i + 2, 2)
-            finish(a, 0)
-            if last:
-                store(a, 0, 512)
-            product(a, 512, bank[1])
-            if not last:
-                each_pass(ret_quantize, i + 1)
-            product(b, 0, bank[2])
-            finish(a, 512)
-            if last:
-                store(a, 512, 512)
-            else:
-                store(a)
-            if not last:
-                product(b, 512, bank[3])
-                finish(b, 0)
-                if i + 2 == PAIRS:
-                    store(b, 0, 512)
-            else:
-                product(b, 512, bank[3], 256)
-                finish(b, 0)
-                store(b, 0, 512)
-                product(b, 768, bank[4], 256)
-                finish(b, 512, 256)
-                store(b, 512, 256)
-                finish(b, 768, 256)
-                store(b, 768, 256)
+        ring = (3, 5, 1, 2, 7, 4, 0, 6)
+        taken = []
+
+        def next_bank():
+            taken.append(ring[len(taken) % len(ring)])
+            return taken[-1]
+
+        def halves_of(tiles):
+            return [(tile, n0) for tile in tiles for n0 in (0, 512)]
+
+        def finish_and_store(tile, n0):
+            finish(tile, n0)
+            if tile >= TILES - 3:
+                store(tile, n0, 512)
+            elif n0:
+                store(tile)
+
+        def scalar_share(i, share):
+            widen_scalar(i, range(share, BLOCKS))
+            ret_split(i, 1, share - 4)
+            if i % 2 == 0:
+                ret_split(i, 2)
+
+        share_a, share_b = 6, 6
+        for job in halves_of((2, 3))[:3]:
+            product(*job, next_bank())
+        finish_and_store(0, 512)
+        widen_vector(3, range(0, 4))
+        finish_and_store(1, 512)
+        widen_vector(3, range(4, share_b))
+        scalar_share(3, share_b)
+        before = halves_of((2, 3))
+        finish_and_store(*before[0])
+        for a in range(2, PAIRS, 2):
+            b = a + 1
+            more = a + 2 < PAIRS
+            jobs = halves_of(range(2 * a, 2 * a + 4))
+            for i in (a, b):
+                claim("ret", i, [next_bank() for g in range(G)])
+                ret_turn(i)
+            copies("ret", a, on_scalar)
+            copies("ret", b, on_scalar)
+            finish_and_store(*before[-3])
+            product(*before[-1], next_bank())
+            ret_quantize(a, 0)
+            finish_and_store(*before[-2])
+            ret_quantize(a, 1)
+            ret_quantize(a, 2)
+            for job in jobs[:4]:
+                product(*job, next_bank())
+            if more:
+                widen_vector(a + 2, range(0, 4))
+                scalar_share(a + 2, share_a)
+            finish_and_store(*before[-1])
+            ret_quantize(b, 0)
+            ret_quantize(b, 1)
+            finish_and_store(*jobs[0])
+            ret_quantize(b, 2)
+            for job in jobs[4:7]:
+                product(*job, next_bank())
+            if more:
+                widen_vector(a + 2, range(4, share_a))
+                scalar_share(b + 2, share_b)
+            finish_and_store(*jobs[1])
+            finish_and_store(*jobs[2])
+            if more:
+                widen_vector(b + 2, range(0, 4))
+            finish_and_store(*jobs[3])
+            if more:
+                widen_vector(b + 2, range(4, share_b))
+            finish_and_store(*jobs[4])
+            before = jobs
+        last = TILES - 1
+        product(last, 512, next_bank(), 256)
+        product(last, 768, next_bank(), 256)
+        finish_and_store(*before[-3])
+        finish_and_store(*before[-2])
+        for n0 in (512, 768):
+            finish(last, n0, 256)
+            store(last, n0, 256)

@@ -351,10 +351,9 @@ def tile_scenario_profit_after_cost_d1_kernel(tc, ret_bytes, ret_scale, pos, rat
         def scalar_share(i, share):
             widen_scalar(i, range(share, BLOCKS))
             ret_split(i, 1, share - 4)
-            if i % 2 == 0:
-                ret_split(i, 2)
+            ret_split(i, 2)
 
-        share_a, share_b = 6, 6
+        share_a, share_b = 6, 7
         for job in halves_of((2, 3))[:3]:
             product(*job, next_bank())
         finish_and_store(0, 512)

@@ -22,6 +22,7 @@ BLOCKS = K // 128
 TILES = T // P
 PAIRS = TILES // 2
 POS_TILES = N // P
+COST_COLUMNS = 48
 
 
 def tile_scenario_profit_after_cost_d1_kernel(tc, ret_bytes, ret_scale, pos, rate, out):
@@ -33,9 +34,9 @@ def tile_scenario_profit_after_cost_d1_kernel(tc, ret_bytes, ret_scale, pos, rat
         ctx.enter_context(tc.manual_schedule())
 
         ident = const.tile([P, P], F32, name="ident")
-        rate_sb = const.tile([P, G, 4], BF16, name="rate_sb")
-        scale_first = const.tile([P, 2, BLOCKS], F32, name="scale_first")
-        scale_rest = const.tile([P, TILES - 2, BLOCKS], F32, name="scale_rest")
+        rate_sb = const.tile([P, G * 4], BF16, name="rate_sb")
+        scale_first = const.tile([P, 4 * BLOCKS], F32, name="scale_first")
+        scale_rest = const.tile([P, (TILES - 4) * BLOCKS], F32, name="scale_rest")
         first_pass = const.tile([P, 512], U8, name="first_pass", align_bytes=64)
         pos_sb = [const.tile([P, K], BF16, name=f"pos_sb{m}", align_bytes=64) for m in range(POS_TILES)]
         ret_u8 = [const.tile([P, 2 * K], U8, name=f"ret_u8_{i}", align_bytes=64) for i in range(PAIRS)]
@@ -45,14 +46,22 @@ def tile_scenario_profit_after_cost_d1_kernel(tc, ret_bytes, ret_scale, pos, rat
             [const.tile([P, 2, 256], I32, name=f"pos_abs{c}_{g}", align_bytes=64) for g in range(G)] for c in range(POS_TILES // 2)
         ]
         cost_col = [const.tile([P, 4], F32, name=f"cost_col{h}") for h in range(2)]
-        cost_bc = const.tile([P, N], F32, name="cost_bc", align_bytes=64)
+        cost_bc = [const.tile([P, 512], F32, name=f"cost_bc{h}", align_bytes=64) for h in range(2)]
 
         bytes_v = ret_bytes.rearrange("(p i s) k -> p i (s k)", i=PAIRS, s=2)
         out_v = out.rearrange("(p i) n -> p i n", i=TILES)
         pos_v = pos.rearrange("(m r) k -> m r k", r=P)
 
-        def new_bank(n):
+        free_banks = [0, 1, 2, 3, 4, 5, 6]
+
+        def named_bank(n):
             return psum.tile([P, 512], F32, name=f"bank{n}", tag=f"bank{n}")
+
+        def next_bank():
+            n = free_banks[0]
+            free_banks.remove(n)
+            free_banks.append(n)
+            return named_bank(n)
 
         def load_pos(m):
             nc.sync.dma_start(out=pos_sb[m][:], in_=pos_v[m])
@@ -62,95 +71,94 @@ def tile_scenario_profit_after_cost_d1_kernel(tc, ret_bytes, ret_scale, pos, rat
 
         planes = {}
         plain = {}
+        unsplit = set()
         banks = {}
-        bank_of = {}
         grouped = {}
-
-        def claim(kind, pair, numbers):
-            for g in range(G):
-                bank_of[kind, pair, g] = numbers[g]
 
         def turn(kind, pair, g, s, halves):
             if (kind, pair, g) not in banks:
-                banks[kind, pair, g] = new_bank(bank_of[kind, pair, g])
+                banks[kind, pair, g] = next_bank()
             for u in range(2):
                 col = 256 * u + P * s
                 nc.tensor.transpose(banks[kind, pair, g][:, col : col + P], halves[u], ident[:])
 
-        def pos_turn(m, passes=range(G)):
+        def pos_turn(m):
             words = pos_sb[m][:].bitcast(F32)
-            for g in passes:
-                turn("pos", m // 2, g, m % 2, [words[:, 256 * g + u : 256 * g + 256 : 2] for u in range(2)])
-
-        def pos_turn_pair(c):
             for g in range(G):
-                pos_turn(2 * c, (g,))
-                pos_turn(2 * c + 1, (g,))
+                turn("pos", m // 2, g, m % 2, [words[:, 256 * g + u : 256 * g + 256 : 2] for u in range(2)])
 
         def ret_turn(i, passes=range(G), tiles=(0, 1)):
             for g in passes:
                 for s in tiles:
-                    if (i, g, s) in planes:
-                        words = planes[i, g, s].bitcast(F32)
-                        turn("ret", i, g, s, [words[:, P * u : P * u + P] for u in range(2)])
-                    else:
+                    if (i, g, s) in unsplit:
                         words = plain[i, g, s].bitcast(F32)
                         turn("ret", i, g, s, [words[:, u::2] for u in range(2)])
+                    else:
+                        words = planes[i, g, s].bitcast(F32)
+                        turn("ret", i, g, s, [words[:, P * u : P * u + P] for u in range(2)])
 
-        def copy_out(kind, pair, g, engine_copy):
-            tile = work.tile([P, 1024], BF16, name="grouped", tag="grouped", bufs=12, align_bytes=64)
+        def copy_out(kind, pair, g, engine_copy=nc.scalar.copy):
+            if (kind, pair) not in grouped:
+                grouped[kind, pair] = work.tile([P, G * 1024], BF16, name="grouped", tag="grouped", bufs=4, align_bytes=64)
             engine_copy(
-                out=tile[:].bitcast(F32).rearrange("p (r u) -> p r u", u=2),
+                out=grouped[kind, pair][:, 1024 * g : 1024 * g + 1024].bitcast(F32).rearrange("p (r u) -> p r u", u=2),
                 in_=banks[kind, pair, g][:].rearrange("p (u r) -> p r u", u=2),
             )
-            grouped[kind, pair, g] = tile
 
-        def pos_quantize(c, g):
+        def copies(kind, pair, passes=range(G)):
+            for g in passes:
+                copy_out(kind, pair, g)
+
+        def pos_quantize(c, passes=range(G)):
             cols = slice(256 * c, 256 * c + 256)
-            nc.vector.quantize_mx(out=pos_q[:, g, cols].bitcast(FP8X4), scales=pos_s[:, g, cols], in_=grouped["pos", c, g][:])
+            for g in passes:
+                nc.vector.quantize_mx(
+                    out=pos_q[:, g, cols].bitcast(FP8X4), scales=pos_s[:, g, cols], in_=grouped["pos", c][:, 1024 * g : 1024 * g + 1024]
+                )
 
-        def pos_absolute(c, g):
-            nc.vector.tensor_scalar(
-                out=pos_abs[c][g][:].rearrange("p u r -> p r u"),
-                in0=grouped["pos", c, g][:].bitcast(I32).rearrange("p (r u) -> p r u", u=2),
-                scalar1=0x7FFF7FFF,
-                scalar2=None,
-                op0=ALU.bitwise_and,
-            )
+        def pos_absolute(c, passes=range(G)):
+            for g in passes:
+                nc.vector.tensor_scalar(
+                    out=pos_abs[c][g][:].rearrange("p u r -> p r u"),
+                    in0=grouped["pos", c][:, 1024 * g : 1024 * g + 1024].bitcast(I32).rearrange("p (r u) -> p r u", u=2),
+                    scalar1=0x7FFF7FFF,
+                    scalar2=None,
+                    op0=ALU.bitwise_and,
+                )
 
-        small = new_bank(7)
+        small = named_bank(7)
 
-        def cost_sum(c, width):
-            rates = rate_sb[:].rearrange("p g t -> p (g t)")
-            for s in range(2):
-                col = 2 * c + s
-                for k in range(4 * G):
-                    g, u, e = k // 4, k // 2 % 2, k % 2
-                    mags = pos_abs[c][g][:, u].bitcast(BF16)
-                    nc.tensor.matmul(
-                        out=small[:, 48 * col : 48 * col + width],
-                        lhsT=mags[:, 256 * s + e : 256 * s + 256 : 2],
-                        rhs=rates[:, k : k + 1].to_broadcast([P, width]),
-                        start=(k == 0),
-                        stop=(k == 4 * G - 1),
-                    )
+        def cost_sum(m, width=COST_COLUMNS):
+            c, s = m // 2, m % 2
+            for k in range(4 * G):
+                g, u, e = k // 4, k // 2 % 2, k % 2
+                mags = pos_abs[c][g][:, u].bitcast(BF16)
+                nc.tensor.matmul(
+                    out=small[:, COST_COLUMNS * m : COST_COLUMNS * m + width],
+                    lhsT=mags[:, 256 * s + e : 256 * s + 256 : 2],
+                    rhs=rate_sb[:, k : k + 1].to_broadcast([P, width]),
+                    start=(k == 0),
+                    stop=(k == 4 * G - 1),
+                )
 
         def cost_column(h):
-            nc.vector.tensor_copy(out=cost_col[h][:], in_=small[:, 192 * h : 192 * h + 192 : 48])
+            first = 4 * COST_COLUMNS * h
+            nc.vector.tensor_copy(out=cost_col[h][:], in_=small[:, first : first + 4 * COST_COLUMNS : COST_COLUMNS])
 
-        def cost_spread(h, n):
-            bank = new_bank(n)
+        def cost_spread(h):
+            bank = next_bank()
             for m in range(4):
                 nc.tensor.transpose(bank[:, P * m : P * m + P], cost_col[h][:, m : m + 1].to_broadcast([P, P]), ident[:])
             banks["spread", h] = bank
 
         def cost_row(h):
-            nc.scalar.copy(out=cost_bc[:, 512 * h : 512 * h + 512], in_=banks["spread", h][:])
+            nc.scalar.copy(out=cost_bc[h][:], in_=banks["spread", h][:])
 
         def scale_of(i, s, b):
-            if i == 0:
-                return scale_first[:, s, b : b + 1]
-            return scale_rest[:, 2 * i + s - 2, b : b + 1]
+            col = (2 * i + s) * BLOCKS + b
+            if i < 2:
+                return scale_first[:, col : col + 1]
+            return scale_rest[:, col - 4 * BLOCKS : col - 4 * BLOCKS + 1]
 
         def ret_block(i, s, b):
             first = K * s + P * b
@@ -181,17 +189,6 @@ def tile_scenario_profit_after_cost_d1_kernel(tc, ret_bytes, ret_scale, pos, rat
                         op0=ALU.mult,
                     )
 
-        def widen_vector_plain(i, blocks, tiles=(0, 1)):
-            for b in blocks:
-                for s in tiles:
-                    nc.vector.tensor_scalar(
-                        out=rows_of(plain, "ret_plain", 4, i, b // 4, s)[:, P * (b % 4) : P * (b % 4) + P],
-                        in0=ret_block(i, s, b),
-                        scalar1=scale_of(i, s, b),
-                        scalar2=None,
-                        op0=ALU.mult,
-                    )
-
         def widen_scalar(i, blocks, tiles=(0, 1)):
             for b in blocks:
                 for s in tiles:
@@ -209,26 +206,33 @@ def tile_scenario_profit_after_cost_d1_kernel(tc, ret_bytes, ret_scale, pos, rat
                 in_=plain[i, g].bitcast(F32).rearrange("r (s p u) -> r s u p", s=2, u=2)[:, :, :, 32 * first :],
             )
 
+        def scalar_share(i, share):
+            widen_scalar(i, range(share, BLOCKS))
+            for g in range(share // 4, G):
+                ret_split(i, g, max(share - 4 * g, 0))
+
         ret_q = {}
         ret_s = {}
 
-        def ret_quantize(i, g):
-            if g == 0:
-                ret_q[i] = work.tile([P, G, 256], U32, name="ret_q", tag="ret_q", bufs=4, align_bytes=64)
-                ret_s[i] = work.tile([P, G, 256], U8, name="ret_s", tag="ret_s", bufs=4, align_bytes=64)
-            nc.vector.quantize_mx(out=ret_q[i][:, g].bitcast(FP8X4), scales=ret_s[i][:, g], in_=grouped["ret", i, g][:])
+        def ret_quantize(i, first=0, last=G):
+            if first == 0:
+                ret_q[i] = work.tile([P, G * 256], U32, name="ret_q", tag="ret_q", bufs=4, align_bytes=64)
+                ret_s[i] = work.tile([P, G * 256], U8, name="ret_s", tag="ret_s", bufs=4, align_bytes=64)
+            cols = slice(256 * first, 256 * last)
+            nc.vector.quantize_mx(out=ret_q[i][:, cols].bitcast(FP8X4), scales=ret_s[i][:, cols], in_=grouped["ret", i][:, 1024 * first : 1024 * last])
 
         sums = {}
         result = {}
 
-        def product(tile, n0, bank, n=512):
+        def product(tile, n0, n=512):
             i, s = tile // 2, tile % 2
-            acc = new_bank(bank)
+            acc = next_bank()
             for g in range(G):
+                rows = slice(256 * g + P * s, 256 * g + P * s + P)
                 nc.tensor.matmul_mx(
                     out=acc[:, 0:n],
-                    lhsT=ret_q[i][:, g, P * s : P * s + P].bitcast(FP8X4),
-                    lhsT_scale=ret_s[i][:, g, P * s : P * s + P],
+                    lhsT=ret_q[i][:, rows].bitcast(FP8X4),
+                    lhsT_scale=ret_s[i][:, rows],
                     rhs=pos_q[:, g, n0 : n0 + n].bitcast(FP8X4),
                     rhs_scale=pos_s[:, g, n0 : n0 + n],
                     start=(g == 0),
@@ -240,43 +244,30 @@ def tile_scenario_profit_after_cost_d1_kernel(tc, ret_bytes, ret_scale, pos, rat
             if tile not in result:
                 result[tile] = const.tile([P, N], F32, name=f"result{tile}", align_bytes=64)
             cols = slice(n0, n0 + n)
-            nc.vector.tensor_tensor(out=result[tile][:, cols], in0=sums[tile, n0][:, 0:n], in1=cost_bc[:, cols], op=ALU.subtract)
+            nc.vector.tensor_tensor(
+                out=result[tile][:, cols], in0=sums[tile, n0][:, 0:n], in1=cost_bc[n0 // 512][:, n0 % 512 : n0 % 512 + n], op=ALU.subtract
+            )
+            if tile >= TILES - 3:
+                nc.sync.dma_start(out=out_v[:, tile, cols], in_=result[tile][:, cols])
+            elif n0:
+                nc.sync.dma_start(out=out_v[:, tile], in_=result[tile][:])
 
-        def store(tile, n0=0, n=N):
-            nc.sync.dma_start(out=out_v[:, tile, n0 : n0 + n], in_=result[tile][:, n0 : n0 + n])
-
-        def each_pass(step, *args):
-            for g in range(G):
-                step(*args, g)
-
-        def copies(kind, pair, engines):
-            for g in range(G):
-                copy_out(kind, pair, g, engines[g])
-
-        vcopy = nc.vector.tensor_copy
-        scopy = nc.scalar.copy
-
-        scale_v = ret_scale.rearrange("(p i) b -> p i b", i=TILES)
-        nc.scalar.dma_start(out=scale_first[:], in_=scale_v[:, 0:2])
+        scale_v = ret_scale.rearrange("(p i) b -> p (i b)", i=TILES)
+        nc.scalar.dma_start(out=scale_first[:], in_=scale_v[:, 0 : 4 * BLOCKS])
         nc.sync.dma_start(out=first_pass[:], in_=bytes_v[:, 0, 0:512])
         load_ret(0, 512, K)
         load_ret(0, K, 2 * K)
-        nc.scalar.dma_start(out=rate_sb[:], in_=rate.rearrange("(g p t) -> p g t", p=P, t=4))
+        nc.scalar.dma_start(out=rate_sb[:].rearrange("p (g t) -> p g t", t=4), in_=rate.rearrange("(g p t) -> p g t", p=P, t=4))
         make_identity(nc, ident[:])
-        for m in range(POS_TILES):
-            if m == 7:
-                nc.sync.dma_start(out=scale_rest[:], in_=scale_v[:, 2:TILES])
+        load_pos(0)
+        load_ret(1)
+        for m in range(1, POS_TILES):
             load_pos(m)
-        for i in range(1, PAIRS):
+        nc.sync.dma_start(out=scale_rest[:], in_=scale_v[:, 4 * BLOCKS :])
+        for i in range(2, PAIRS):
             load_ret(i)
-        on_scalar = (scopy, scopy, scopy)
 
-        claim("ret", 0, (0, 1, 2))
-        claim("pos", 0, (3, 4, 5))
-        claim("pos", 1, (6, 0, 1))
-        claim("pos", 2, (2, 3, 4))
-        claim("pos", 3, (5, 6, 0))
-        claim("ret", 1, (3, 4, 5))
+        unsplit.add((0, 2, 0))
         widen_scalar(0, range(8, 12), (0,))
         widen_vector(0, range(0, 8), (0,))
         widen_vector(0, range(0, 12), (1,))
@@ -284,129 +275,150 @@ def tile_scenario_profit_after_cost_d1_kernel(tc, ret_bytes, ret_scale, pos, rat
         ret_turn(0, (0, 1), (1,))
         pos_turn(0)
         ret_turn(0, (2,), (1, 0))
-        copies("ret", 0, (scopy, vcopy, scopy))
-        each_pass(ret_quantize, 0)
-        for m in range(1, POS_TILES):
-            c = m // 2
-            if m == 7:
-                cost_sum(0, 48)
-            pos_turn(m)
-            if m % 2 == 1:
-                copies("pos", c, on_scalar)
-                if c < 2:
-                    each_pass(pos_absolute, c)
-                    each_pass(pos_quantize, c)
-        widen_vector(1, (8, 9))
-        widen_vector(1, range(0, 8))
+        copy_out("ret", 0, 0)
+        copy_out("ret", 0, 1, nc.vector.tensor_copy)
         widen_scalar(1, range(10, 12))
+        copy_out("ret", 0, 2)
+        widen_vector(1, range(0, 8))
+        pos_turn(1)
+        copies("pos", 0)
+        ret_quantize(0, 0, 2)
+        ret_quantize(0, 2)
+        pos_absolute(0, (0, 1))
+        widen_vector(1, range(8, 10))
+        pos_absolute(0, (2,))
+        pos_quantize(0)
+        ret_turn(1, (0,))
+        pos_turn(2)
+        copies("ret", 1, (0,))
+        pos_turn(3)
+        copies("pos", 1)
         ret_split(1, 2, 2)
-        cost_sum(1, 48)
-        product(0, 0, 1)
-        product(1, 0, 2)
+        pos_absolute(1)
+        pos_quantize(1)
+        pos_turn(4)
+        pos_turn(5)
+        copies("pos", 2)
+        pos_turn(6)
+        cost_sum(0)
+        cost_sum(1)
+        ret_quantize(1, 0, 1)
+        pos_absolute(2)
+        pos_turn(7)
+        widen_scalar(2, range(10, 12))
+        copies("pos", 3)
+        cost_sum(2)
+        cost_sum(3)
+        pos_quantize(2, (0,))
         cost_column(0)
-        each_pass(pos_quantize, 2)
-        each_pass(pos_absolute, 2)
-        each_pass(pos_quantize, 3)
-        each_pass(pos_absolute, 3)
-        ret_turn(1)
-        cost_spread(0, 6)
-        cost_sum(2, 48)
-        widen_scalar(2, range(6, 8))
-        copy_out("ret", 1, 0, scopy)
+        pos_quantize(2, (1, 2))
+        widen_vector(2, range(0, 4))
+        ret_turn(1, (1, 2))
+        cost_spread(0)
+        pos_absolute(3)
+        copies("ret", 1, (1, 2))
         cost_row(0)
-        copy_out("ret", 1, 1, scopy)
-        copy_out("ret", 1, 2, scopy)
-        product(0, 512, 0)
-        cost_sum(3, 48)
+        cost_sum(4, 1)
+        cost_sum(5, 1)
+        product(0, 0)
+        product(1, 0)
+        widen_vector(2, range(4, 8))
+        ret_quantize(1, 1)
+        cost_sum(6, 1)
+        cost_sum(7, 1)
         finish(0, 0)
-        widen_vector(2, range(0, 3))
         cost_column(1)
-        product(1, 512, 6)
-        each_pass(ret_quantize, 1)
-        cost_spread(1, 4)
-        widen_vector(2, range(3, 6))
-        widen_scalar(2, range(8, 12))
-        ret_split(2, 1, 2)
-        cost_row(1)
+        widen_scalar(2, range(8, 10))
+        widen_scalar(3, range(10, 12))
         ret_split(2, 2)
+        product(2, 0)
+        product(3, 0)
+        pos_quantize(3)
         finish(1, 0)
-
-        ring = (3, 5, 1, 2, 7, 4, 0, 6)
-        taken = []
-
-        def next_bank():
-            taken.append(ring[len(taken) % len(ring)])
-            return taken[-1]
+        free_banks.append(7)
+        widen_scalar(3, range(7, 10))
+        cost_spread(1)
+        ret_turn(2)
+        cost_row(1)
+        copies("ret", 2)
+        finish(2, 0)
+        widen_vector(3, range(0, 4))
+        finish(3, 0)
+        product(0, 512)
+        product(1, 512)
+        widen_vector(3, range(4, 7))
+        finish(0, 512)
+        ret_quantize(2, 0, 2)
+        ret_split(3, 1, 3)
+        ret_split(3, 2)
+        product(2, 512)
+        product(3, 512)
+        finish(1, 512)
+        ret_quantize(2, 2)
+        product(4, 0)
+        product(4, 512)
+        scalar_share(4, 6)
+        finish(2, 512)
+        widen_vector(4, range(0, 6))
+        finish(3, 512)
 
         def halves_of(tiles):
             return [(tile, n0) for tile in tiles for n0 in (0, 512)]
 
-        def finish_and_store(tile, n0):
-            finish(tile, n0)
-            if tile >= TILES - 3:
-                store(tile, n0, 512)
-            elif n0:
-                store(tile)
-
-        def scalar_share(i, share):
-            widen_scalar(i, range(share, BLOCKS))
-            ret_split(i, 1, share - 4)
-            ret_split(i, 2)
-
-        share_a, share_b = 6, 7
-        for job in halves_of((2, 3))[:3]:
-            product(*job, next_bank())
-        finish_and_store(0, 512)
-        widen_vector(3, range(0, 4))
-        finish_and_store(1, 512)
-        widen_vector(3, range(4, share_b))
-        scalar_share(3, share_b)
-        before = halves_of((2, 3))
-        finish_and_store(*before[0])
-        for a in range(2, PAIRS, 2):
+        before = halves_of((4, 5))
+        for a, share_a, share_b in ((3, 6, 7), (5, 3, None)):
             b = a + 1
-            more = a + 2 < PAIRS
             jobs = halves_of(range(2 * a, 2 * a + 4))
-            for i in (a, b):
-                claim("ret", i, [next_bank() for g in range(G)])
-                ret_turn(i)
-            copies("ret", a, on_scalar)
-            copies("ret", b, on_scalar)
-            finish_and_store(*before[-3])
-            product(*before[-1], next_bank())
-            ret_quantize(a, 0)
-            finish_and_store(*before[-2])
-            ret_quantize(a, 1)
+            ret_turn(a)
+            ret_turn(b)
+            copies("ret", a)
+            copies("ret", b)
+            finish(*before[-4])
+            finish(*before[-3])
+            product(*before[-2])
+            product(*before[-1])
+            ret_quantize(a, 0, 2)
+            widen_vector(a + 2, range(0, 2))
             ret_quantize(a, 2)
             for job in jobs[:4]:
-                product(*job, next_bank())
-            if more:
-                widen_vector(a + 2, range(0, 4))
-                scalar_share(a + 2, share_a)
-            finish_and_store(*before[-1])
-            ret_quantize(b, 0)
-            ret_quantize(b, 1)
-            finish_and_store(*jobs[0])
+                product(*job)
+            finish(*before[-2])
+            ret_quantize(b, 0, 2)
+            finish(*before[-1])
             ret_quantize(b, 2)
-            for job in jobs[4:7]:
-                product(*job, next_bank())
-            if more:
-                widen_vector(a + 2, range(4, share_a))
+            widen_vector(a + 2, range(2, share_a))
+            scalar_share(a + 2, share_a)
+            finish(*jobs[0])
+            for job in jobs[4:6]:
+                product(*job)
+            if share_b:
                 scalar_share(b + 2, share_b)
-            finish_and_store(*jobs[1])
-            finish_and_store(*jobs[2])
-            if more:
                 widen_vector(b + 2, range(0, 4))
-            finish_and_store(*jobs[3])
-            if more:
+            finish(*jobs[1])
+            finish(*jobs[2])
+            if share_b:
                 widen_vector(b + 2, range(4, share_b))
-            finish_and_store(*jobs[4])
+            finish(*jobs[3])
             before = jobs
-        last = TILES - 1
-        product(last, 512, next_bank(), 256)
-        product(last, 768, next_bank(), 256)
-        finish_and_store(*before[-3])
-        finish_and_store(*before[-2])
-        for n0 in (512, 768):
-            finish(last, n0, 256)
-            store(last, n0, 256)
+        last = PAIRS - 1
+        ret_turn(last)
+        copies("ret", last)
+        finish(*before[4])
+        finish(*before[5])
+        product(*before[-2])
+        product(*before[-1])
+        ret_quantize(last, 0, 1)
+        ret_quantize(last, 1, 2)
+        ret_quantize(last, 2)
+        finish(*before[6])
+        product(14, 0)
+        product(14, 512)
+        product(15, 0)
+        product(15, 512, 256)
+        product(15, 768, 256)
+        finish(*before[7])
+        finish(14, 0)
+        finish(14, 512)
+        finish(15, 0)
+        finish(15, 512, 256)
+        finish(15, 768, 256)

@@ -82,10 +82,23 @@ def tile_scenario_profit_after_cost_d1_kernel(tc, ret_bytes, ret_scale, pos, rat
                 col = 256 * u + P * s
                 nc.tensor.transpose(banks[kind, pair, g][:, col : col + P], halves[u], ident[:])
 
+        pos_planes = {}
+
+        def pos_split(m, engine_copy=nc.vector.tensor_copy):
+            pos_planes[m] = work.tile([P, K // 2], F32, name="pos_planes", tag="pos_planes", bufs=4, align_bytes=64)
+            engine_copy(
+                out=pos_planes[m][:].rearrange("r (g u p) -> r g u p", g=G, u=2),
+                in_=pos_sb[m][:].bitcast(F32).rearrange("r (g p u) -> r g u p", g=G, u=2),
+            )
+
         def pos_turn(m):
             words = pos_sb[m][:].bitcast(F32)
             for g in range(G):
-                turn("pos", m // 2, g, m % 2, [words[:, 256 * g + u : 256 * g + 256 : 2] for u in range(2)])
+                if m in pos_planes:
+                    halves = [pos_planes[m][:, 256 * g + P * u : 256 * g + P * u + P] for u in range(2)]
+                else:
+                    halves = [words[:, 256 * g + u : 256 * g + 256 : 2] for u in range(2)]
+                turn("pos", m // 2, g, m % 2, halves)
 
         def ret_turn(i, passes=range(G), tiles=(0, 1)):
             for g in passes:
@@ -99,7 +112,7 @@ def tile_scenario_profit_after_cost_d1_kernel(tc, ret_bytes, ret_scale, pos, rat
 
         def copy_out(kind, pair, g, engine_copy=nc.scalar.copy):
             if (kind, pair) not in grouped:
-                grouped[kind, pair] = work.tile([P, G * 1024], BF16, name="grouped", tag="grouped", bufs=4, align_bytes=64)
+                grouped[kind, pair] = work.tile([P, G * 1024], BF16, name="grouped", tag="grouped", bufs=5, align_bytes=64)
             engine_copy(
                 out=grouped[kind, pair][:, 1024 * g : 1024 * g + 1024].bitcast(F32).rearrange("p (r u) -> p r u", u=2),
                 in_=banks[kind, pair, g][:].rearrange("p (u r) -> p r u", u=2),
@@ -199,11 +212,11 @@ def tile_scenario_profit_after_cost_d1_kernel(tc, ret_bytes, ret_scale, pos, rat
                         scale=scale_of(i, s, b),
                     )
 
-        def ret_split(i, g, first=0):
+        def ret_split(i, g, first=0, last=4):
             rows_of(planes, "ret_planes", 9, i, g, 0)
             nc.scalar.copy(
-                out=planes[i, g].bitcast(F32).rearrange("r (s u p) -> r s u p", s=2, u=2)[:, :, :, 32 * first :],
-                in_=plain[i, g].bitcast(F32).rearrange("r (s p u) -> r s u p", s=2, u=2)[:, :, :, 32 * first :],
+                out=planes[i, g].bitcast(F32).rearrange("r (s u p) -> r s u p", s=2, u=2)[:, :, :, 32 * first : 32 * last],
+                in_=plain[i, g].bitcast(F32).rearrange("r (s p u) -> r s u p", s=2, u=2)[:, :, :, 32 * first : 32 * last],
             )
 
         def scalar_share(i, share):
@@ -242,7 +255,7 @@ def tile_scenario_profit_after_cost_d1_kernel(tc, ret_bytes, ret_scale, pos, rat
 
         def finish(tile, n0, n=512):
             if tile not in result:
-                result[tile] = const.tile([P, N], F32, name=f"result{tile}", align_bytes=64)
+                result[tile] = work.tile([P, N], F32, name="result", tag="result", bufs=10, align_bytes=64)
             cols = slice(n0, n0 + n)
             nc.vector.tensor_tensor(
                 out=result[tile][:, cols], in0=sums[tile, n0][:, 0:n], in1=cost_bc[n0 // 512][:, n0 % 512 : n0 % 512 + n], op=ALU.subtract

from contextlib import ExitStack

import concourse.mybir as mybir
from concourse.masks import make_identity

T, K, N = 2048, 1536, 1024
FLOPS = 2 * T * K * N + 3 * N * K

F32 = mybir.dt.float32
BF16 = mybir.dt.bfloat16
U32 = mybir.dt.uint32
I32 = mybir.dt.int32
U8 = mybir.dt.uint8
FP8 = mybir.dt.float8_e4m3fn
FP8X4 = mybir.dt.float8_e4m3fn_x4
ALU = mybir.AluOpType
COPY = mybir.ActivationFunctionType.Copy

P = 128
G = K // 512
BLOCKS = K // 128
TILES = T // P
PAIRS = TILES // 2
POS_TILES = N // P
COST_COLUMNS = 48


def tile_scenario_profit_after_cost_d1_kernel(tc, ret_bytes, ret_scale, pos, rate, out):
    nc = tc.nc
    with ExitStack() as ctx:
        const = ctx.enter_context(tc.tile_pool(name="const", bufs=1))
        work = ctx.enter_context(tc.tile_pool(name="work", bufs=3))
        psum = ctx.enter_context(tc.psum_pool(name="psum", bufs=1))
        ctx.enter_context(tc.manual_schedule())

        ident = const.tile([P, P], F32, name="ident")
        rate_sb = const.tile([P, G * 4], BF16, name="rate_sb")
        scale_first = const.tile([P, 4 * BLOCKS], F32, name="scale_first")
        scale_rest = const.tile([P, (TILES - 4) * BLOCKS], F32, name="scale_rest")
        first_pass = const.tile([P, 512], U8, name="first_pass", align_bytes=64)
        pos_sb = [const.tile([P, K], BF16, name=f"pos_sb{m}", align_bytes=64) for m in range(POS_TILES)]
        ret_u8 = [const.tile([P, 2 * K], U8, name=f"ret_u8_{i}", align_bytes=64) for i in range(PAIRS)]
        pos_q = const.tile([P, G, N], U32, name="pos_q", align_bytes=64)
        pos_s = const.tile([P, G, N], U8, name="pos_s", align_bytes=64)
        pos_abs = [
            [const.tile([P, 2, 256], I32, name=f"pos_abs{c}_{g}", align_bytes=64) for g in range(G)] for c in range(POS_TILES // 2)
        ]
        cost_col = [const.tile([P, 4], F32, name=f"cost_col{h}") for h in range(2)]
        cost_bc = [const.tile([P, 512], F32, name=f"cost_bc{h}", align_bytes=64) for h in range(2)]

        bytes_v = ret_bytes.rearrange("(p i s) k -> p i (s k)", i=PAIRS, s=2)
        out_v = out.rearrange("(p i) n -> p i n", i=TILES)
        pos_v = pos.rearrange("(m r) k -> m r k", r=P)

        free_banks = [0, 1, 2, 3, 4, 5, 6]

        def named_bank(n):
            return psum.tile([P, 512], F32, name=f"bank{n}", tag=f"bank{n}")

        def next_bank():
            n = free_banks[0]
            free_banks.remove(n)
            free_banks.append(n)
            return named_bank(n)

        def load_pos(m):
            nc.sync.dma_start(out=pos_sb[m][:], in_=pos_v[m])

        def load_ret(i, first=0, last=2 * K):
            nc.sync.dma_start(out=ret_u8[i][:, first:last], in_=bytes_v[:, i, first:last])

        planes = {}
        plain = {}
        unsplit = set()
        banks = {}
        grouped = {}

        def turn(kind, pair, g, s, halves):
            if (kind, pair, g) not in banks:
                banks[kind, pair, g] = next_bank()
            for u in range(2):
                col = 256 * u + P * s
                nc.tensor.transpose(banks[kind, pair, g][:, col : col + P], halves[u], ident[:])

        pos_planes = {}

        def pos_split(m, engine_copy=nc.vector.tensor_copy):
            pos_planes[m] = work.tile([P, K // 2], F32, name="pos_planes", tag="pos_planes", bufs=4, align_bytes=64)
            engine_copy(
                out=pos_planes[m][:].rearrange("r (g u p) -> r g u p", g=G, u=2),
                in_=pos_sb[m][:].bitcast(F32).rearrange("r (g p u) -> r g u p", g=G, u=2),
            )

        def pos_turn(m):
            words = pos_sb[m][:].bitcast(F32)
            for g in range(G):
                if m in pos_planes:
                    halves = [pos_planes[m][:, 256 * g + P * u : 256 * g + P * u + P] for u in range(2)]
                else:
                    halves = [words[:, 256 * g + u : 256 * g + 256 : 2] for u in range(2)]
                turn("pos", m // 2, g, m % 2, halves)

        def ret_turn(i, passes=range(G), tiles=(0, 1)):
            for g in passes:
                for s in tiles:
                    if (i, g, s) in unsplit:
                        words = plain[i, g, s].bitcast(F32)
                        turn("ret", i, g, s, [words[:, u::2] for u in range(2)])
                    else:
                        words = planes[i, g, s].bitcast(F32)
                        turn("ret", i, g, s, [words[:, P * u : P * u + P] for u in range(2)])

        def copy_out(kind, pair, g, engine_copy=nc.scalar.copy):
            if (kind, pair) not in grouped:
                grouped[kind, pair] = work.tile([P, G * 1024], BF16, name="grouped", tag="grouped", bufs=5, align_bytes=64)
            engine_copy(
                out=grouped[kind, pair][:, 1024 * g : 1024 * g + 1024].bitcast(F32).rearrange("p (r u) -> p r u", u=2),
                in_=banks[kind, pair, g][:].rearrange("p (u r) -> p r u", u=2),
            )

        def copies(kind, pair, passes=range(G)):
            for g in passes:
                copy_out(kind, pair, g)

        def pos_quantize(c, passes=range(G)):
            cols = slice(256 * c, 256 * c + 256)
            for g in passes:
                nc.vector.quantize_mx(
                    out=pos_q[:, g, cols].bitcast(FP8X4), scales=pos_s[:, g, cols], in_=grouped["pos", c][:, 1024 * g : 1024 * g + 1024]
                )

        def pos_absolute(c, passes=range(G)):
            for g in passes:
                nc.vector.tensor_scalar(
                    out=pos_abs[c][g][:].rearrange("p u r -> p r u"),
                    in0=grouped["pos", c][:, 1024 * g : 1024 * g + 1024].bitcast(I32).rearrange("p (r u) -> p r u", u=2),
                    scalar1=0x7FFF7FFF,
                    scalar2=None,
                    op0=ALU.bitwise_and,
                )

        small = named_bank(7)

        def cost_sum(m, width=COST_COLUMNS):
            c, s = m // 2, m % 2
            for k in range(4 * G):
                g, u, e = k // 4, k // 2 % 2, k % 2
                mags = pos_abs[c][g][:, u].bitcast(BF16)
                nc.tensor.matmul(
                    out=small[:, COST_COLUMNS * m : COST_COLUMNS * m + width],
                    lhsT=mags[:, 256 * s + e : 256 * s + 256 : 2],
                    rhs=rate_sb[:, k : k + 1].to_broadcast([P, width]),
                    start=(k == 0),
                    stop=(k == 4 * G - 1),
                )

        def cost_column(h):
            first = 4 * COST_COLUMNS * h
            nc.vector.tensor_copy(out=cost_col[h][:], in_=small[:, first : first + 4 * COST_COLUMNS : COST_COLUMNS])

        def cost_spread(h):
            bank = next_bank()
            for m in range(4):
                nc.tensor.transpose(bank[:, P * m : P * m + P], cost_col[h][:, m : m + 1].to_broadcast([P, P]), ident[:])
            banks["spread", h] = bank

        def cost_row(h):
            nc.scalar.copy(out=cost_bc[h][:], in_=banks["spread", h][:])

        def scale_of(i, s, b):
            col = (2 * i + s) * BLOCKS + b
            if i < 2:
                return scale_first[:, col : col + 1]
            return scale_rest[:, col - 4 * BLOCKS : col - 4 * BLOCKS + 1]

        def ret_block(i, s, b):
            first = K * s + P * b
            if i == 0 and first < 512:
                return first_pass[:, first : first + P].bitcast(FP8)
            return ret_u8[i][:, first : first + P].bitcast(FP8)

        def rows_of(store, name, bufs, i, g, s):
            if i == 0:
                if (i, g, s) not in store:
                    store[i, g, s] = const.tile([P, 512], BF16, name=f"first_{name}{g}_{s}", align_bytes=64)[:]
            elif (i, g, s) not in store:
                both = work.tile([P, 1024], BF16, name=name, tag=name, bufs=bufs, align_bytes=64)
                store[i, g] = both[:]
                store[i, g, 0] = both[:, 0:512]
                store[i, g, 1] = both[:, 512:1024]
            return store[i, g, s]

        def widen_vector(i, blocks, tiles=(0, 1)):
            for b in blocks:
                for s in tiles:
                    dst = rows_of(planes, "ret_planes", 9, i, b // 4, s).rearrange("r (u p e) -> r p u e", u=2, e=2)
                    nc.vector.tensor_scalar(
                        out=dst[:, 32 * (b % 4) : 32 * (b % 4) + 32],
                        in0=ret_block(i, s, b).rearrange("r (p u e) -> r p u e", u=2, e=2),
                        scalar1=scale_of(i, s, b),
                        scalar2=None,
                        op0=ALU.mult,
                    )

        def widen_scalar(i, blocks, tiles=(0, 1)):
            for b in blocks:
                for s in tiles:
                    nc.scalar.activation(
                        out=rows_of(plain, "ret_plain", 4, i, b // 4, s)[:, P * (b % 4) : P * (b % 4) + P],
                        in_=ret_block(i, s, b),
                        func=COPY,
                        scale=scale_of(i, s, b),
                    )

        def ret_split(i, g, first=0, last=4):
            rows_of(planes, "ret_planes", 9, i, g, 0)
            nc.scalar.copy(
                out=planes[i, g].bitcast(F32).rearrange("r (s u p) -> r s u p", s=2, u=2)[:, :, :, 32 * first : 32 * last],
                in_=plain[i, g].bitcast(F32).rearrange("r (s p u) -> r s u p", s=2, u=2)[:, :, :, 32 * first : 32 * last],
            )

        def scalar_share(i, share):
            widen_scalar(i, range(share, BLOCKS))
            for g in range(share // 4, G):
                ret_split(i, g, max(share - 4 * g, 0))

        ret_q = {}
        ret_s = {}

        def ret_quantize(i, first=0, last=G):
            if first == 0:
                ret_q[i] = work.tile([P, G * 256], U32, name="ret_q", tag="ret_q", bufs=4, align_bytes=64)
                ret_s[i] = work.tile([P, G * 256], U8, name="ret_s", tag="ret_s", bufs=4, align_bytes=64)
            cols = slice(256 * first, 256 * last)
            nc.vector.quantize_mx(out=ret_q[i][:, cols].bitcast(FP8X4), scales=ret_s[i][:, cols], in_=grouped["ret", i][:, 1024 * first : 1024 * last])

        sums = {}
        result = {}

        def product(tile, n0, n=512):
            i, s = tile // 2, tile % 2
            acc = next_bank()
            for g in range(G):
                rows = slice(256 * g + P * s, 256 * g + P * s + P)
                nc.tensor.matmul_mx(
                    out=acc[:, 0:n],
                    lhsT=ret_q[i][:, rows].bitcast(FP8X4),
                    lhsT_scale=ret_s[i][:, rows],
                    rhs=pos_q[:, g, n0 : n0 + n].bitcast(FP8X4),
                    rhs_scale=pos_s[:, g, n0 : n0 + n],
                    start=(g == 0),
                    stop=(g == G - 1),
                )
            sums[tile, n0] = acc

        def finish(tile, n0, n=512):
            if tile not in result:
                result[tile] = work.tile([P, N], F32, name="result", tag="result", bufs=10, align_bytes=64)
            cols = slice(n0, n0 + n)
            nc.vector.tensor_tensor(
                out=result[tile][:, cols], in0=sums[tile, n0][:, 0:n], in1=cost_bc[n0 // 512][:, n0 % 512 : n0 % 512 + n], op=ALU.subtract
            )
            if tile >= TILES - 3:
                nc.sync.dma_start(out=out_v[:, tile, cols], in_=result[tile][:, cols])
            elif n0:
                nc.sync.dma_start(out=out_v[:, tile], in_=result[tile][:])

        scale_v = ret_scale.rearrange("(p i) b -> p (i b)", i=TILES)
        nc.scalar.dma_start(out=scale_first[:], in_=scale_v[:, 0 : 4 * BLOCKS])
        nc.sync.dma_start(out=first_pass[:], in_=bytes_v[:, 0, 0:512])
        load_ret(0, 512, K)
        load_ret(0, K, 2 * K)
        nc.scalar.dma_start(out=rate_sb[:].rearrange("p (g t) -> p g t", t=4), in_=rate.rearrange("(g p t) -> p g t", p=P, t=4))
        make_identity(nc, ident[:])
        load_pos(0)
        load_ret(1)
        for m in range(1, POS_TILES):
            load_pos(m)
        nc.sync.dma_start(out=scale_rest[:], in_=scale_v[:, 4 * BLOCKS :])
        for i in range(2, PAIRS):
            load_ret(i)

        unsplit.add((0, 2, 0))
        widen_scalar(0, range(8, 12), (0,))
        widen_vector(0, range(0, 8), (0,))
        widen_vector(0, range(0, 12), (1,))
        ret_turn(0, (0, 1), (0,))
        ret_turn(0, (0, 1), (1,))
        pos_turn(0)
        ret_turn(0, (2,), (1, 0))
        copy_out("ret", 0, 0)
        copy_out("ret", 0, 1, nc.vector.tensor_copy)
        widen_scalar(1, range(10, 12))
        copy_out("ret", 0, 2)
        widen_vector(1, range(0, 8))
        pos_turn(1)
        copies("pos", 0)
        ret_quantize(0, 0, 2)
        ret_quantize(0, 2)
        pos_absolute(0, (0, 1))
        widen_vector(1, range(8, 10))
        pos_absolute(0, (2,))
        pos_quantize(0)
        ret_turn(1, (0,))
        pos_turn(2)
        copies("ret", 1, (0,))
        pos_turn(3)
        copies("pos", 1)
        ret_split(1, 2, 2)
        pos_absolute(1)
        pos_quantize(1)
        pos_turn(4)
        pos_turn(5)
        copies("pos", 2)
        pos_turn(6)
        cost_sum(0)
        cost_sum(1)
        ret_quantize(1, 0, 1)
        pos_absolute(2)
        pos_turn(7)
        widen_scalar(2, range(10, 12))
        copies("pos", 3)
        cost_sum(2)
        cost_sum(3)
        pos_quantize(2, (0,))
        cost_column(0)
        pos_quantize(2, (1, 2))
        widen_vector(2, range(0, 4))
        ret_turn(1, (1, 2))
        cost_spread(0)
        pos_absolute(3)
        copies("ret", 1, (1, 2))
        cost_row(0)
        cost_sum(4, 1)
        cost_sum(5, 1)
        product(0, 0)
        product(1, 0)
        widen_vector(2, range(4, 8))
        ret_quantize(1, 1)
        cost_sum(6, 1)
        cost_sum(7, 1)
        finish(0, 0)
        cost_column(1)
        widen_scalar(2, range(8, 10))
        widen_scalar(3, range(10, 12))
        ret_split(2, 2)
        product(2, 0)
        product(3, 0)
        pos_quantize(3)
        finish(1, 0)
        free_banks.append(7)
        widen_scalar(3, range(7, 10))
        cost_spread(1)
        ret_turn(2)
        cost_row(1)
        copies("ret", 2)
        finish(2, 0)
        widen_vector(3, range(0, 4))
        finish(3, 0)
        product(0, 512)
        product(1, 512)
        widen_vector(3, range(4, 7))
        finish(0, 512)
        ret_quantize(2, 0, 2)
        ret_split(3, 1, 3)
        ret_split(3, 2)
        product(2, 512)
        product(3, 512)
        finish(1, 512)
        ret_quantize(2, 2)
        product(4, 0)
        product(4, 512)
        scalar_share(4, 6)
        finish(2, 512)
        widen_vector(4, range(0, 6))
        finish(3, 512)

        def halves_of(tiles):
            return [(tile, n0) for tile in tiles for n0 in (0, 512)]

        before = halves_of((4, 5))
        for a, share_a, share_b in ((3, 6, 7), (5, 3, None)):
            b = a + 1
            jobs = halves_of(range(2 * a, 2 * a + 4))
            ret_turn(a)
            ret_turn(b)
            copies("ret", a)
            copies("ret", b)
            finish(*before[-4])
            finish(*before[-3])
            product(*before[-2])
            product(*before[-1])
            ret_quantize(a, 0, 2)
            widen_vector(a + 2, range(0, 2))
            ret_quantize(a, 2)
            for job in jobs[:4]:
                product(*job)
            finish(*before[-2])
            ret_quantize(b, 0, 2)
            finish(*before[-1])
            ret_quantize(b, 2)
            widen_vector(a + 2, range(2, share_a))
            scalar_share(a + 2, share_a)
            finish(*jobs[0])
            for job in jobs[4:6]:
                product(*job)
            if share_b:
                scalar_share(b + 2, share_b)
                widen_vector(b + 2, range(0, 4))
            finish(*jobs[1])
            finish(*jobs[2])
            if share_b:
                widen_vector(b + 2, range(4, share_b))
            finish(*jobs[3])
            before = jobs
        last = PAIRS - 1
        ret_turn(last)
        copies("ret", last)
        finish(*before[4])
        finish(*before[5])
        product(*before[-2])
        product(*before[-1])
        ret_quantize(last, 0, 1)
        ret_quantize(last, 1, 2)
        ret_quantize(last, 2)
        finish(*before[6])
        product(14, 0)
        product(14, 512)
        product(15, 0)
        product(15, 512, 256)
        product(15, 768, 256)
        finish(*before[7])
        finish(14, 0)
        finish(14, 512)
        finish(15, 0)
        finish(15, 512, 256)
        finish(15, 768, 256)
